import numpy as np
import ml_dtypes


def mxq(x, axis, fmt="e4m3"):
    dtype, down = {"e4m3": (ml_dtypes.float8_e4m3fn, 7), "e5m2": (ml_dtypes.float8_e5m2, 14)}[fmt]
    v = np.moveaxis(np.asarray(x, np.float32).astype(ml_dtypes.bfloat16).astype(np.float64), axis, -1)
    blocks = v.reshape(v.shape[:-1] + (-1, 32))
    amax = np.abs(blocks).max(-1, keepdims=True)
    byte = np.maximum(np.where(amax > 0, np.frexp(amax)[1] - 1 + 127, 0) - down, 1)
    scale = np.exp2(byte - 127.0)
    codes = (blocks / scale).astype(np.float32).astype(dtype).astype(np.float64)
    return np.moveaxis((codes * scale).reshape(v.shape), -1, axis)


WIDE = False


def mx_kscale(k):
    if not WIDE:
        return np.ones(k)
    levels = np.array([10, -10, 5, -5, 0])
    if k % 512:
        return np.exp2(np.random.permutation(np.resize(levels, k // 32))).repeat(32)
    a = np.empty((k // 512, 16))
    for p in range(k // 512):
        a[p, :8] = np.random.permutation(np.resize(levels, 8))
        for g in range(8):
            far = levels[np.abs(levels - a[p, g]) >= 10]
            a[p, g + 8] = far[np.random.randint(len(far))]
    return np.exp2(a.ravel()).repeat(32)


def f64(x):
    return np.asarray(x).astype(np.float64)


def striped(idx):
    return np.tile(idx.reshape(-1, 16).T, (8, 1)).astype(np.uint16)


def unstriped(offs):
    return offs[:16].T.reshape(-1).astype(np.int64)


def pack_weight(w):
    k, n = w.shape
    w = f64(np.asarray(w, np.float32).astype(ml_dtypes.bfloat16)).reshape(k // 32, 32, n)
    amax = np.abs(w).max(1)
    byte = np.clip(np.where(amax > 0, np.frexp(amax)[1] - 1 + 127 - 7, 1), 1, 254)
    scaled = (w * np.exp2(127.0 - byte)[:, None, :]).reshape(k, n).astype(np.float32)
    words = np.ascontiguousarray(scaled.reshape(k // 512, 128, 4, n).transpose(0, 1, 3, 2)).astype(ml_dtypes.float8_e4m3fn).view(np.uint8)
    return words, np.ascontiguousarray(byte.astype(np.uint8).reshape(k // 512, 16, n))


def unpack_weight(words, scales):
    g, p, n, _ = words.shape
    vals = np.ascontiguousarray(words).view(ml_dtypes.float8_e4m3fn).astype(np.float64) * np.repeat(np.exp2(scales.astype(np.float64) - 127.0), 8, axis=1)[..., None]
    return vals.transpose(0, 1, 3, 2).reshape(g * 512, n)


def sigmoid(v):
    return 1.0 / (1.0 + np.exp(-np.maximum(v, -700.0)))


K, T, S, H, D, V, W, U = 1024, 2048, 512, 512, 2, 256, 1024, 512
P = 2 ** 7


def setup_inputs():
    n = np.random.standard_normal
    s = mx_kscale(K)[:, None]
    u = mx_kscale(H)
    packed_xT = pack_weight(n((K, T)) * s)
    packed_eT = pack_weight(n((H, W)) / np.sqrt(H) / u[:, None])
    return {
        "x_words": packed_xT[0],
        "x_scales": packed_xT[1],
        "w1": (n((K, H)) / np.sqrt(K) / s * u).astype(np.float32),
        "e_words": packed_eT[0],
        "e_scales": packed_eT[1],
        "gain": (np.tile(np.random.uniform(0.5, 1.0, V), (P, 1))).astype(np.float32),
        "offs": striped(np.random.permutation(T)[:S]),
        "pos": striped(np.random.permutation(W)[:V]),
        "neg": striped(np.random.permutation(W)[:U]),
    }


def reference(x_words, x_scales, w1, e_words, e_scales, gain, offs, pos, neg):
    xq = unpack_weight(x_words, x_scales)[:, unstriped(offs)]
    h = mxq(f64(w1), 0, "e4m3").T @ xq
    hq = mxq(h, 0, "e4m3")
    e_neg = unpack_weight(e_words, e_scales)[:, unstriped(neg)]
    z = hq.T @ e_neg
    e_pos = unpack_weight(e_words, e_scales)[:, unstriped(pos)]
    y = hq.T @ e_pos
    gg = sigmoid(4.0 * (z - np.repeat(y, D, axis=1)))
    rr = gg.reshape(len(gg), -1, D).sum(axis=2)
    return f64(gain)[:1] / (rr + 1.0)

@@ -1,0 +1,226 @@
+from contextlib import ExitStack
+
+import concourse.mybir as mybir
+
+K, T, S, H, V, W, U = 1024, 2048, 512, 512, 256, 1024, 512
+FLOPS = 2 * K * H * S + 2 * H * S * (U + V)
+
+F32 = mybir.dt.float32
+BF16 = mybir.dt.bfloat16
+I32 = mybir.dt.int32
+U32 = mybir.dt.uint32
+U16 = mybir.dt.uint16
+U8 = mybir.dt.uint8
+FP8X4 = mybir.dt.float8_e4m3fn_x4
+ACT = mybir.ActivationFunctionType
+ALU = mybir.AluOpType
+
+P = 128
+PACK = 4
+PASSES = K // (P * PACK)
+TILES = S // P
+HALVES = 2
+CHUNKS = 4
+
+
+def tile_picked_ysmap_gain_p_kernel(
+    tc, x_words, x_scales, w1, e_words, e_scales, gain, offs, pos, neg, out
+):
+    nc = tc.nc
+    with ExitStack() as ctx:
+        sb = ctx.enter_context(tc.tile_pool(name="sb", bufs=1))
+        psum = ctx.enter_context(tc.psum_pool(name="psum", bufs=1))
+
+        def sbuf(name, shape, dtype):
+            return sb.tile(shape, dtype, name=name, align_bytes=64)
+
+        offs_t = sbuf("offs_t", [P, S // 16], U16)
+        pos_t = sbuf("pos_t", [P, V // 16], U16)
+        neg_t = sbuf("neg_t", [P, U // 16], U16)
+        ew = sbuf("ew", [P, W], I32)
+        es = sbuf("es", [P, W], U8)
+        xs = sbuf("xs", [P, T], U8)
+        xw = [sbuf("xw%d" % g, [P, T], I32) for g in range(PASSES)]
+        HC = H // HALVES
+        wraw = [[sbuf("wraw%d%d" % (g, a), [P, PACK, HC], F32) for a in range(HALVES)] for g in range(PASSES)]
+        gain_t = sbuf("gain_t", [P, V], F32)
+
+        warm_in = sbuf("warm_in", [P, 1], F32)
+        warm_out = sbuf("warm_out", [P, 1], F32)
+        nc.gpsimd.memset(warm_in[:], 0.0)
+        nc.scalar.activation(out=warm_out[:], in_=warm_in[:], func=ACT.Sigmoid)
+
+        nc.vector.memset(es[:].bitcast(I32), 0)
+        nc.vector.memset(xs[:].bitcast(I32), 0)
+
+        def load_w(g, a):
+            rows = w1[512 * g : 512 * (g + 1), HC * a : HC * (a + 1)]
+            nc.sync.dma_start(out=wraw[g][a][:], in_=rows.rearrange("(p r) c -> p r c", r=PACK))
+
+        def load_x(g):
+            nc.sync.dma_start(out=xw[g][:], in_=x_words[g].rearrange("p n t -> p (n t)").bitcast(I32))
+
+        nc.sync.dma_start(neg_t[:], neg)
+        nc.sync.dma_start(pos_t[:], pos)
+        nc.sync.dma_start(out=ew[:], in_=e_words[0].rearrange("p n t -> p (n t)").bitcast(I32))
+        load_w(0, 0)
+        for q in range(4):
+            nc.scalar.dma_start(
+                out=es[32 * q : 32 * q + 4, :].bitcast(I32), in_=e_scales[0, 4 * q : 4 * q + 4, :].bitcast(I32)
+            )
+        load_w(0, 1)
+        load_w(1, 0)
+        nc.sync.dma_start(offs_t[:], offs)
+        for q in range(4):
+            nc.scalar.dma_start(
+                out=xs[32 * q : 32 * q + 8, :].bitcast(I32), in_=x_scales[:, 4 * q : 4 * q + 4, :].bitcast(I32)
+            )
+        load_x(0)
+        load_w(1, 1)
+        load_x(1)
+        nc.sync.dma_start(out=gain_t[:], in_=gain)
+
+        negw_g = sbuf("negw_g", [P, U], U32)
+        negs_g = sbuf("negs_g", [P, U], U8)
+        posw = sbuf("posw", [P, V], U32)
+        poss = sbuf("poss", [P, V], U8)
+        negw = sbuf("negw", [P, U], U32)
+        negs = sbuf("negs", [P, U], U8)
+        nc.vector.tensor_copy(out=negw_g[:], in_=ew[:].bitcast(U32).indirect(neg_t[:]))
+        nc.vector.tensor_copy(out=posw[:], in_=ew[:].bitcast(U32).indirect(pos_t[:]))
+        nc.vector.tensor_copy(out=negs_g[:], in_=es[:].indirect(neg_t[:]))
+        nc.vector.tensor_copy(out=poss[:], in_=es[:].indirect(pos_t[:]))
+        nc.vector.tensor_copy(
+            out=negw[:].rearrange("p (d v) -> p v d", d=2), in_=negw_g[:].rearrange("p (v d) -> p v d", d=2)
+        )
+        nc.vector.tensor_copy(
+            out=negs[:].rearrange("p (d v) -> p v d", d=2), in_=negs_g[:].rearrange("p (v d) -> p v d", d=2)
+        )
+
+        wb = [sbuf("wb%d" % g, [P, PACK, P, PACK], BF16) for g in range(PASSES)]
+        wq = [sbuf("wq%d" % g, [P, H], U32) for g in range(PASSES)]
+        wsc = [sbuf("wsc%d" % g, [P, H], U8) for g in range(PASSES)]
+        MH = P // HALVES
+
+        def cast_w(g, a):
+            nc.scalar.copy(
+                out=wb[g][:, :, MH * a : MH * (a + 1), :].rearrange("p j m r -> p m r j"),
+                in_=wraw[g][a][:].rearrange("p r (m j) -> p m r j", j=PACK),
+            )
+
+        def quant_w(g):
+            nc.vector.quantize_mx(
+                out=wq[g][:].bitcast(FP8X4), scales=wsc[g][:], in_=wb[g][:].rearrange("p j m r -> p (j m r)")
+            )
+
+        xsg = sbuf("xsg", [P, S], U8)
+        SH = S // 2
+        xg = [[sbuf("xg%d%d" % (g, a), [P, SH], U32) for a in range(2)] for g in range(PASSES)]
+
+        def gather_x(g, a):
+            cols = slice(a * SH // 16, (a + 1) * SH // 16)
+            nc.vector.tensor_copy(out=xg[g][a][:], in_=xw[g][:].bitcast(U32).indirect(offs_t[:, cols]))
+
+        hb = [psum.tile([P, PACK, P], F32, name="hb%d" % i) for i in range(TILES)]
+        zb = [psum.tile([P, U], F32, name="zb%d" % i) for i in range(TILES)]
+
+        def project(g, i):
+            a, b = divmod(i, 2)
+            for j in range(PACK):
+                nc.tensor.matmul_mx(
+                    out=hb[i][:, j, :],
+                    lhsT=wq[g][:, P * j : P * (j + 1)].bitcast(FP8X4),
+                    lhsT_scale=wsc[g][:, P * j : P * (j + 1)],
+                    rhs=xg[g][a][:, P * b : P * (b + 1)].bitcast(FP8X4),
+                    rhs_scale=xsg[4 * g :, P * i : P * (i + 1)],
+                    start=(g == 0 and j == 0),
+                    stop=(g == PASSES - 1 and j == PACK - 1),
+                )
+
+        for g in range(PASSES):
+            for a in range(HALVES):
+                cast_w(g, a)
+        quant_w(0)
+        nc.vector.tensor_copy(out=xsg[:], in_=xs[:].indirect(offs_t[:]))
+        gather_x(0, 0)
+        gather_x(0, 1)
+        for i in range(TILES):
+            project(0, i)
+        quant_w(1)
+        gather_x(1, 0)
+        gather_x(1, 1)
+
+        hp = [sbuf("hp%d" % i, [P, H], BF16) for i in range(TILES)]
+        hn = [sbuf("hn%d" % i, [P, H], BF16) for i in range(TILES)]
+        hpq = [sbuf("hpq%d" % i, [P, P], U32) for i in range(TILES)]
+        hps = [sbuf("hps%d" % i, [P, P], U8) for i in range(TILES)]
+        hnq = [sbuf("hnq%d" % i, [P, P], U32) for i in range(TILES)]
+        hns = [sbuf("hns%d" % i, [P, P], U8) for i in range(TILES)]
+        sg = [sbuf("sg%d" % i, [P, U], F32) for i in range(TILES)]
+        rank = sbuf("rank", [P, TILES, V], F32)
+
+        def drain(i):
+            engine_copy = nc.vector.tensor_copy if i == 1 else nc.scalar.copy
+            engine_copy(out=hp[i][:].rearrange("p (t j) -> p t j", j=PACK), in_=hb[i][:].rearrange("p j t -> p t j"))
+
+        def quant_plus(i):
+            nc.vector.quantize_mx(out=hpq[i][:].bitcast(FP8X4), scales=hps[i][:], in_=hp[i][:])
+
+        def negate(i):
+            nc.vector.tensor_scalar(out=hn[i][:], in0=hp[i][:], scalar1=-1.0, scalar2=None, op0=ALU.mult)
+
+        def quant_minus(i):
+            nc.vector.quantize_mx(out=hnq[i][:].bitcast(FP8X4), scales=hns[i][:], in_=hn[i][:])
+
+        def score(i):
+            nc.tensor.matmul_mx(
+                out=zb[i][:], lhsT=hpq[i][:].bitcast(FP8X4), lhsT_scale=hps[i][:],
+                rhs=negw[:].bitcast(FP8X4), rhs_scale=negs[:], start=True, stop=False,
+            )
+            for d in range(2):
+                nc.tensor.matmul_mx(
+                    out=zb[i][:, V * d : V * (d + 1)], lhsT=hnq[i][:].bitcast(FP8X4), lhsT_scale=hns[i][:],
+                    rhs=posw[:].bitcast(FP8X4), rhs_scale=poss[:], start=False, stop=(d == 1),
+                )
+            nc.scalar.activation(out=sg[i][:], in_=zb[i][:], func=ACT.Sigmoid, scale=4.0)
+
+        def add_up(i):
+            nc.vector.scalar_tensor_tensor(
+                out=rank[:, i, :], in0=sg[i][:, 0:V], scalar=1.0, in1=sg[i][:, V : 2 * V], op0=ALU.add, op1=ALU.add
+            )
+
+        for i in range(TILES):
+            project(1, i)
+            drain(i)
+        for i in range(TILES):
+            negate(i)
+            quant_plus(i)
+            quant_minus(i)
+            score(i)
+        for i in range(TILES):
+            add_up(i)
+
+        out_v = out.rearrange("(i p) v -> p i v", p=P)
+        res = sbuf("res", [P, TILES, V], F32)
+        RW, CW = 32, 56
+        cols = [slice(RW + CW * c, RW + CW * (c + 1)) for c in range(CHUNKS)]
+
+        def gains(lo, width):
+            return gain_t[:, lo : lo + width].unsqueeze(1).to_broadcast([P, TILES, width])
+
+        inv = sbuf("inv", [P, TILES, RW], F32)
+        nc.vector.reciprocal(out=inv[:], in_=rank[:, :, 0:RW])
+        nc.vector.tensor_tensor(out=res[:, :, 0:RW], in0=inv[:], in1=gains(0, RW), op=ALU.mult)
+        root = [sbuf("root%d" % c, [P, TILES, CW], F32) for c in range(CHUNKS)]
+        part = [sbuf("part%d" % c, [P, TILES, CW], F32) for c in range(CHUNKS)]
+        for c in range(CHUNKS):
+            nc.scalar.activation(out=root[c][:], in_=rank[:, :, cols[c]], func=ACT.Abs_reciprocal_sqrt)
+        for c in (0, 1):
+            nc.vector.tensor_tensor(out=part[c][:], in0=root[c][:], in1=gains(cols[c].start, CW), op=ALU.mult)
+        for c in (0, 1):
+            nc.vector.tensor_tensor(out=res[:, :, cols[c]], in0=part[c][:], in1=root[c][:], op=ALU.mult)
+        nc.sync.dma_start(out=out_v[:, :, 0 : cols[1].stop], in_=res[:, :, 0 : cols[1].stop])
+        for c in (2, 3):
+            nc.scalar.activation(out=part[c][:], in_=root[c][:], func=ACT.Square)
+            nc.vector.tensor_tensor(out=res[:, :, cols[c]], in0=part[c][:], in1=gains(cols[c].start, CW), op=ALU.mult)
+            nc.sync.dma_start(out=out_v[:, :, cols[c]], in_=res[:, :, cols[c]])

@@ -20,7 +20,7 @@ PACK = 4
 PASSES = K // (P * PACK)
 TILES = S // P
 HALVES = 2
-CHUNKS = 4
+E_ROW = 8
 
 
 def tile_picked_ysmap_gain_p_kernel(
@@ -39,44 +39,46 @@ def tile_picked_ysmap_gain_p_kernel(
         neg_t = sbuf("neg_t", [P, U // 16], U16)
         ew = sbuf("ew", [P, W], I32)
         es = sbuf("es", [P, W], U8)
-        xs = sbuf("xs", [P, T], U8)
+        xs = sb.tile([P, T], U8, name="xs", tag="x_scale_bytes", align_bytes=64)
         xw = [sbuf("xw%d" % g, [P, T], I32) for g in range(PASSES)]
         HC = H // HALVES
-        wraw = [[sbuf("wraw%d%d" % (g, a), [P, PACK, HC], F32) for a in range(HALVES)] for g in range(PASSES)]
+        wraw = [sbuf("wraw%d" % g, [P, PACK, H], F32) for g in range(PASSES)]
         gain_t = sbuf("gain_t", [P, V], F32)
 
         warm_in = sbuf("warm_in", [P, 1], F32)
         warm_out = sbuf("warm_out", [P, 1], F32)
-        nc.gpsimd.memset(warm_in[:], 0.0)
+        nc.vector.memset(warm_in[:], 0.0)
         nc.scalar.activation(out=warm_out[:], in_=warm_in[:], func=ACT.Sigmoid)
 
-        nc.vector.memset(es[:].bitcast(I32), 0)
+        nc.gpsimd.memset(es[:].bitcast(I32), 0)
         nc.vector.memset(xs[:].bitcast(I32), 0)
 
-        def load_w(g, a):
-            rows = w1[512 * g : 512 * (g + 1), HC * a : HC * (a + 1)]
-            nc.sync.dma_start(out=wraw[g][a][:], in_=rows.rearrange("(p r) c -> p r c", r=PACK))
+        def load_w(g):
+            rows = w1[512 * g : 512 * (g + 1), :]
+            nc.sync.dma_start(out=wraw[g][:], in_=rows.rearrange("(p r) c -> p r c", r=PACK))
 
         def load_x(g):
             nc.sync.dma_start(out=xw[g][:], in_=x_words[g].rearrange("p n t -> p (n t)").bitcast(I32))
 
+        def load_xs(n):
+            g, q = divmod(n, 4)
+            lo = 32 * q + 4 * g
+            nc.sync.dma_start(out=xs[lo : lo + 4, :].bitcast(I32), in_=x_scales[g, 4 * q : 4 * q + 4, :].bitcast(I32))
+
+        nc.sync.dma_start(out=ew[:], in_=e_words[0].rearrange("p n t -> p (n t)").bitcast(I32))
         nc.sync.dma_start(neg_t[:], neg)
         nc.sync.dma_start(pos_t[:], pos)
-        nc.sync.dma_start(out=ew[:], in_=e_words[0].rearrange("p n t -> p (n t)").bitcast(I32))
-        load_w(0, 0)
         for q in range(4):
-            nc.scalar.dma_start(
-                out=es[32 * q : 32 * q + 4, :].bitcast(I32), in_=e_scales[0, 4 * q : 4 * q + 4, :].bitcast(I32)
-            )
-        load_w(0, 1)
-        load_w(1, 0)
+            lo = 32 * q + E_ROW
+            nc.sync.dma_start(out=es[lo : lo + 4, :].bitcast(I32), in_=e_scales[0, 4 * q : 4 * q + 4, :].bitcast(I32))
+        load_w(0)
         nc.sync.dma_start(offs_t[:], offs)
-        for q in range(4):
-            nc.scalar.dma_start(
-                out=xs[32 * q : 32 * q + 8, :].bitcast(I32), in_=x_scales[:, 4 * q : 4 * q + 4, :].bitcast(I32)
-            )
+        for n in range(3):
+            load_xs(n)
         load_x(0)
-        load_w(1, 1)
+        for n in range(3, 8):
+            load_xs(n)
+        load_w(1)
         load_x(1)
         nc.sync.dma_start(out=gain_t[:], in_=gain)
 
@@ -100,22 +102,26 @@ def tile_picked_ysmap_gain_p_kernel(
         wb = [sbuf("wb%d" % g, [P, PACK, P, PACK], BF16) for g in range(PASSES)]
         wq = [sbuf("wq%d" % g, [P, H], U32) for g in range(PASSES)]
         wsc = [sbuf("wsc%d" % g, [P, H], U8) for g in range(PASSES)]
-        MH = P // HALVES
 
-        def cast_w(g, a):
-            nc.scalar.copy(
-                out=wb[g][:, :, MH * a : MH * (a + 1), :].rearrange("p j m r -> p m r j"),
-                in_=wraw[g][a][:].rearrange("p r (m j) -> p m r j", j=PACK),
+        def cast_w(copy, g, a):
+            copy(
+                out=wb[g][:, 2 * a : 2 * a + 2, :, :].rearrange("p j m r -> p m r j"),
+                in_=wraw[g][:].rearrange("p r (m j) -> p m r j", j=PACK)[:, :, :, 2 * a : 2 * a + 2],
             )
 
-        def quant_w(g):
+        def quant_w(g, a):
             nc.vector.quantize_mx(
-                out=wq[g][:].bitcast(FP8X4), scales=wsc[g][:], in_=wb[g][:].rearrange("p j m r -> p (j m r)")
+                out=wq[g][:, HC * a : HC * (a + 1)].bitcast(FP8X4),
+                scales=wsc[g][:, HC * a : HC * (a + 1)],
+                in_=wb[g][:, 2 * a : 2 * a + 2, :, :].rearrange("p j m r -> p (j m r)"),
             )
 
         xsg = sbuf("xsg", [P, S], U8)
         SH = S // 2
-        xg = [[sbuf("xg%d%d" % (g, a), [P, SH], U32) for a in range(2)] for g in range(PASSES)]
+        xg = [
+            [sb.tile([P, SH], U32, name="xg00", tag="x_scale_bytes", align_bytes=64), sbuf("xg01", [P, SH], U32)],
+            [sbuf("xg10", [P, SH], U32), sbuf("xg11", [P, SH], U32)],
+        ]
 
         def gather_x(g, a):
             cols = slice(a * SH // 16, (a + 1) * SH // 16)
@@ -137,50 +143,52 @@ def tile_picked_ysmap_gain_p_kernel(
                     stop=(g == PASSES - 1 and j == PACK - 1),
                 )
 
-        for g in range(PASSES):
-            for a in range(HALVES):
-                cast_w(g, a)
-        quant_w(0)
+        for a in range(HALVES):
+            cast_w(nc.scalar.copy, 0, a)
+            quant_w(0, a)
         nc.vector.tensor_copy(out=xsg[:], in_=xs[:].indirect(offs_t[:]))
         gather_x(0, 0)
         gather_x(0, 1)
         for i in range(TILES):
             project(0, i)
-        quant_w(1)
+        cast_w(nc.vector.tensor_copy, 1, 0)
+        cast_w(nc.scalar.copy, 1, 1)
+        quant_w(1, 0)
+        quant_w(1, 1)
         gather_x(1, 0)
         gather_x(1, 1)
 
-        hp = [sbuf("hp%d" % i, [P, H], BF16) for i in range(TILES)]
-        hn = [sbuf("hn%d" % i, [P, H], BF16) for i in range(TILES)]
-        hpq = [sbuf("hpq%d" % i, [P, P], U32) for i in range(TILES)]
-        hps = [sbuf("hps%d" % i, [P, P], U8) for i in range(TILES)]
-        hnq = [sbuf("hnq%d" % i, [P, P], U32) for i in range(TILES)]
-        hns = [sbuf("hns%d" % i, [P, P], U8) for i in range(TILES)]
-        sg = [sbuf("sg%d" % i, [P, U], F32) for i in range(TILES)]
+        hb16 = [[sbuf("hb16_%d%d" % (i, sign), [P, H], BF16) for sign in range(2)] for i in range(TILES - 1)]
+        hb16.append([sbuf("hb16_30", [P, H], BF16), sb.tile([P, H], BF16, name="hb16_31", tag="h_last", align_bytes=64)])
+        hq = [[sbuf("hq%d%d" % (i, sign), [P, P], U32) for sign in range(2)] for i in range(TILES)]
+        hs = [[sbuf("hs%d%d" % (i, sign), [P, P], U8) for sign in range(2)] for i in range(TILES)]
+        sg = [sbuf("sg%d" % i, [P, U], F32) for i in range(TILES - 1)]
+        sg.append(sb.tile([P, U], F32, name="sg_last", tag="late", align_bytes=64))
         rank = sbuf("rank", [P, TILES, V], F32)
 
         def drain(i):
             engine_copy = nc.vector.tensor_copy if i == 1 else nc.scalar.copy
-            engine_copy(out=hp[i][:].rearrange("p (t j) -> p t j", j=PACK), in_=hb[i][:].rearrange("p j t -> p t j"))
-
-        def quant_plus(i):
-            nc.vector.quantize_mx(out=hpq[i][:].bitcast(FP8X4), scales=hps[i][:], in_=hp[i][:])
+            engine_copy(out=hb16[i][0][:].rearrange("p (t j) -> p t j", j=PACK), in_=hb[i][:].rearrange("p j t -> p t j"))
 
         def negate(i):
-            nc.vector.tensor_scalar(out=hn[i][:], in0=hp[i][:], scalar1=-1.0, scalar2=None, op0=ALU.mult)
+            nc.vector.tensor_scalar(
+                out=hb16[i][1][:], in0=hb16[i][0][:], scalar1=-1.0, scalar2=None, op0=ALU.mult
+            )
 
-        def quant_minus(i):
-            nc.vector.quantize_mx(out=hnq[i][:].bitcast(FP8X4), scales=hns[i][:], in_=hn[i][:])
+        def quant_h(i, sign):
+            nc.vector.quantize_mx(
+                out=hq[i][sign][:].bitcast(FP8X4), scales=hs[i][sign][:], in_=hb16[i][sign][:]
+            )
 
         def score(i):
             nc.tensor.matmul_mx(
-                out=zb[i][:], lhsT=hpq[i][:].bitcast(FP8X4), lhsT_scale=hps[i][:],
-                rhs=negw[:].bitcast(FP8X4), rhs_scale=negs[:], start=True, stop=False,
+                out=zb[i][:], lhsT=hq[i][0][:].bitcast(FP8X4), lhsT_scale=hs[i][0][:],
+                rhs=negw[:].bitcast(FP8X4), rhs_scale=negs[E_ROW:, :], start=True, stop=False,
             )
             for d in range(2):
                 nc.tensor.matmul_mx(
-                    out=zb[i][:, V * d : V * (d + 1)], lhsT=hnq[i][:].bitcast(FP8X4), lhsT_scale=hns[i][:],
-                    rhs=posw[:].bitcast(FP8X4), rhs_scale=poss[:], start=False, stop=(d == 1),
+                    out=zb[i][:, V * d : V * (d + 1)], lhsT=hq[i][1][:].bitcast(FP8X4), lhsT_scale=hs[i][1][:],
+                    rhs=posw[:].bitcast(FP8X4), rhs_scale=poss[E_ROW:, :], start=False, stop=(d == 1),
                 )
             nc.scalar.activation(out=sg[i][:], in_=zb[i][:], func=ACT.Sigmoid, scale=4.0)
 
@@ -194,33 +202,35 @@ def tile_picked_ysmap_gain_p_kernel(
             drain(i)
         for i in range(TILES):
             negate(i)
-            quant_plus(i)
-            quant_minus(i)
+            quant_h(i, 0)
+            quant_h(i, 1)
             score(i)
         for i in range(TILES):
             add_up(i)
 
-        out_v = out.rearrange("(i p) v -> p i v", p=P)
+        RW = 192
+        root = sb.tile([P, TILES, V], F32, name="root", tag="late", align_bytes=64)
+        part = sbuf("part", [P, TILES, V], F32)
         res = sbuf("res", [P, TILES, V], F32)
-        RW, CW = 32, 56
-        cols = [slice(RW + CW * c, RW + CW * (c + 1)) for c in range(CHUNKS)]
 
-        def gains(lo, width):
-            return gain_t[:, lo : lo + width].unsqueeze(1).to_broadcast([P, TILES, width])
+        def times(dst, a, b):
+            nc.vector.tensor_tensor(out=dst, in0=a, in1=b, op=ALU.mult)
 
-        inv = sbuf("inv", [P, TILES, RW], F32)
-        nc.vector.reciprocal(out=inv[:], in_=rank[:, :, 0:RW])
-        nc.vector.tensor_tensor(out=res[:, :, 0:RW], in0=inv[:], in1=gains(0, RW), op=ALU.mult)
-        root = [sbuf("root%d" % c, [P, TILES, CW], F32) for c in range(CHUNKS)]
-        part = [sbuf("part%d" % c, [P, TILES, CW], F32) for c in range(CHUNKS)]
-        for c in range(CHUNKS):
-            nc.scalar.activation(out=root[c][:], in_=rank[:, :, cols[c]], func=ACT.Abs_reciprocal_sqrt)
-        for c in (0, 1):
-            nc.vector.tensor_tensor(out=part[c][:], in0=root[c][:], in1=gains(cols[c].start, CW), op=ALU.mult)
-        for c in (0, 1):
-            nc.vector.tensor_tensor(out=res[:, :, cols[c]], in0=part[c][:], in1=root[c][:], op=ALU.mult)
-        nc.sync.dma_start(out=out_v[:, :, 0 : cols[1].stop], in_=res[:, :, 0 : cols[1].stop])
-        for c in (2, 3):
-            nc.scalar.activation(out=part[c][:], in_=root[c][:], func=ACT.Square)
-            nc.vector.tensor_tensor(out=res[:, :, cols[c]], in0=part[c][:], in1=gains(cols[c].start, CW), op=ALU.mult)
-            nc.sync.dma_start(out=out_v[:, :, cols[c]], in_=res[:, :, cols[c]])
+        def store(i, cols=slice(0, V)):
+            nc.sync.dma_start(out=out[P * i : P * (i + 1), cols], in_=res[:, i, cols])
+
+        inv = sb.tile([P, RW], F32, name="inv", tag="h_last", align_bytes=64)
+        nc.vector.reciprocal(out=inv[:], in_=rank[:, 0, 0:RW])
+        times(res[:, 0, 0:RW], inv[:], gain_t[:, 0:RW])
+        first = [RW, 0, 0, 0]
+        for i in range(TILES):
+            nc.scalar.activation(out=root[:, i, first[i] :], in_=rank[:, i, first[i] :], func=ACT.Abs_reciprocal_sqrt)
+        for i in (0, 1):
+            times(part[:, i, first[i] :], root[:, i, first[i] :], gain_t[:, first[i] :])
+        for i in (0, 1):
+            times(res[:, i, first[i] :], part[:, i, first[i] :], root[:, i, first[i] :])
+            store(i)
+        for i, cols in ((2, slice(0, V)), (3, slice(0, V // 2)), (3, slice(V // 2, V))):
+            nc.scalar.activation(out=part[:, i, cols], in_=root[:, i, cols], func=ACT.Square)
+            times(res[:, i, cols], part[:, i, cols], gain_t[:, cols])
+            store(i, cols)

@@ -61,16 +61,14 @@ def tile_picked_ysmap_gain_p_kernel(
             nc.sync.dma_start(out=xw[g][:], in_=x_words[g].rearrange("p n t -> p (n t)").bitcast(I32))
 
         def load_xs(n):
-            g, q = divmod(n, 4)
-            lo = 32 * q + 4 * g
-            nc.sync.dma_start(out=xs[lo : lo + 4, :].bitcast(I32), in_=x_scales[g, 4 * q : 4 * q + 4, :].bitcast(I32))
+            r, g = divmod(n, PASSES)
+            nc.sync.dma_start(out=xs[4 * g + r : P : 32, :].bitcast(I32), in_=x_scales[g, r:16:4, :].bitcast(I32))
 
         nc.sync.dma_start(out=ew[:], in_=e_words[0].rearrange("p n t -> p (n t)").bitcast(I32))
         nc.sync.dma_start(neg_t[:], neg)
         nc.sync.dma_start(pos_t[:], pos)
-        for q in range(4):
-            lo = 32 * q + E_ROW
-            nc.sync.dma_start(out=es[lo : lo + 4, :].bitcast(I32), in_=e_scales[0, 4 * q : 4 * q + 4, :].bitcast(I32))
+        for r in range(4):
+            nc.sync.dma_start(out=es[E_ROW + r : P : 32, :].bitcast(I32), in_=e_scales[0, r:16:4, :].bitcast(I32))
         load_w(0)
         nc.sync.dma_start(offs_t[:], offs)
         for n in range(3):
@@ -230,7 +228,7 @@ def tile_picked_ysmap_gain_p_kernel(
         for i in (0, 1):
             times(res[:, i, first[i] :], part[:, i, first[i] :], root[:, i, first[i] :])
             store(i)
-        for i, cols in ((2, slice(0, V)), (3, slice(0, V // 2)), (3, slice(V // 2, V))):
+        for i, cols in ((2, slice(0, V)), (3, slice(0, V))):
             nc.scalar.activation(out=part[:, i, cols], in_=root[:, i, cols], func=ACT.Square)
             times(res[:, i, cols], part[:, i, cols], gain_t[:, cols])
             store(i, cols)

@@ -125,7 +125,7 @@ def tile_picked_ysmap_gain_p_kernel(
             cols = slice(a * SH // 16, (a + 1) * SH // 16)
             nc.vector.tensor_copy(out=xg[g][a][:], in_=xw[g][:].bitcast(U32).indirect(offs_t[:, cols]))
 
-        hb = [psum.tile([P, PACK, P], F32, name="hb%d" % i) for i in range(TILES)]
+        hb = [psum.tile([P, PACK, P], F32, name="hb%d" % i, tag="bank%d" % i) for i in range(TILES)]
         zb = [psum.tile([P, U], F32, name="zb%d" % i) for i in range(TILES)]
 
         def project(g, i):
@@ -178,17 +178,19 @@ def tile_picked_ysmap_gain_p_kernel(
                 out=hq[i][sign][:].bitcast(FP8X4), scales=hs[i][sign][:], in_=hb16[i][sign][:]
             )
 
-        def score(i):
-            nc.tensor.matmul_mx(
-                out=zb[i][:], lhsT=hq[i][0][:].bitcast(FP8X4), lhsT_scale=hs[i][0][:],
-                rhs=negw[:].bitcast(FP8X4), rhs_scale=negs[E_ROW:, :], start=True, stop=False,
-            )
+        def score_halves(i, spare):
+            banks = [zb[i][:, 0:V], psum.tile([P, V], F32, name="z_second%d" % i, tag=spare)[:]]
             for d in range(2):
                 nc.tensor.matmul_mx(
-                    out=zb[i][:, V * d : V * (d + 1)], lhsT=hq[i][1][:].bitcast(FP8X4), lhsT_scale=hs[i][1][:],
-                    rhs=posw[:].bitcast(FP8X4), rhs_scale=poss[E_ROW:, :], start=False, stop=(d == 1),
+                    out=banks[d], lhsT=hq[i][0][:].bitcast(FP8X4), lhsT_scale=hs[i][0][:],
+                    rhs=negw[:, V * d : V * (d + 1)].bitcast(FP8X4), rhs_scale=negs[E_ROW:, V * d : V * (d + 1)],
+                    start=True, stop=False,
                 )
-            nc.scalar.activation(out=sg[i][:], in_=zb[i][:], func=ACT.Sigmoid, scale=4.0)
+                nc.tensor.matmul_mx(
+                    out=banks[d], lhsT=hq[i][1][:].bitcast(FP8X4), lhsT_scale=hs[i][1][:],
+                    rhs=posw[:].bitcast(FP8X4), rhs_scale=poss[E_ROW:, :], start=False, stop=True,
+                )
+                nc.scalar.activation(out=sg[i][:, V * d : V * (d + 1)], in_=banks[d], func=ACT.Sigmoid, scale=4.0)
 
         def add_up(i):
             nc.vector.scalar_tensor_tensor(
@@ -202,11 +204,15 @@ def tile_picked_ysmap_gain_p_kernel(
             negate(i)
             quant_h(i, 0)
             quant_h(i, 1)
-            score(i)
-        for i in range(TILES):
+            score_halves(i, "bank%d" % i)
+        RW = V
+        inv = sb.tile([P, RW], F32, name="inv", tag="h_last", align_bytes=64)
+        add_up(0)
+        nc.vector.reciprocal(out=inv[:, 0 : RW // 2], in_=rank[:, 0, 0 : RW // 2])
+        for i in range(1, TILES):
             add_up(i)
+        nc.vector.reciprocal(out=inv[:, RW // 2 : RW], in_=rank[:, 0, RW // 2 : RW])
 
-        RW = 192
         root = sb.tile([P, TILES, V], F32, name="root", tag="late", align_bytes=64)
         part = sbuf("part", [P, TILES, V], F32)
         res = sbuf("res", [P, TILES, V], F32)
@@ -217,17 +223,13 @@ def tile_picked_ysmap_gain_p_kernel(
         def store(i, cols=slice(0, V)):
             nc.sync.dma_start(out=out[P * i : P * (i + 1), cols], in_=res[:, i, cols])
 
-        inv = sb.tile([P, RW], F32, name="inv", tag="h_last", align_bytes=64)
-        nc.vector.reciprocal(out=inv[:], in_=rank[:, 0, 0:RW])
-        times(res[:, 0, 0:RW], inv[:], gain_t[:, 0:RW])
-        first = [RW, 0, 0, 0]
-        for i in range(TILES):
-            nc.scalar.activation(out=root[:, i, first[i] :], in_=rank[:, i, first[i] :], func=ACT.Abs_reciprocal_sqrt)
-        for i in (0, 1):
-            times(part[:, i, first[i] :], root[:, i, first[i] :], gain_t[:, first[i] :])
-        for i in (0, 1):
-            times(res[:, i, first[i] :], part[:, i, first[i] :], root[:, i, first[i] :])
-            store(i)
+        for i in range(1, TILES):
+            nc.scalar.activation(out=root[:, i, :], in_=rank[:, i, :], func=ACT.Abs_reciprocal_sqrt)
+        times(part[:, 1, :], root[:, 1, :], gain_t[:])
+        times(res[:, 0, :], inv[:], gain_t[:])
+        store(0)
+        times(res[:, 1, :], part[:, 1, :], root[:, 1, :])
+        store(1)
         for i, cols in ((2, slice(0, V)), (3, slice(0, V))):
             nc.scalar.activation(out=part[:, i, cols], in_=root[:, i, cols], func=ACT.Square)
             times(res[:, i, cols], part[:, i, cols], gain_t[:, cols])

@@ -19,8 +19,13 @@ P = 128
 PACK = 4
 PASSES = K // (P * PACK)
 TILES = S // P
-HALVES = 2
-E_ROW = 8
+D = 2
+LIST = 16
+QUADRANT = 32
+E_FIRST = 8
+XS_AHEAD = 3
+VECTOR_BANK = 1
+RECIP_COLS = 64
 
 
 def tile_picked_ysmap_gain_p_kernel(
@@ -31,206 +36,227 @@ def tile_picked_ysmap_gain_p_kernel(
         sb = ctx.enter_context(tc.tile_pool(name="sb", bufs=1))
         psum = ctx.enter_context(tc.psum_pool(name="psum", bufs=1))
 
-        def sbuf(name, shape, dtype):
-            return sb.tile(shape, dtype, name=name, align_bytes=64)
+        def sbuf(name, shape, dtype, tag=None):
+            return sb.tile(shape, dtype, name=name, tag=tag or name, align_bytes=64)
 
-        offs_t = sbuf("offs_t", [P, S // 16], U16)
-        pos_t = sbuf("pos_t", [P, V // 16], U16)
-        neg_t = sbuf("neg_t", [P, U // 16], U16)
-        ew = sbuf("ew", [P, W], I32)
-        es = sbuf("es", [P, W], U8)
-        xs = sb.tile([P, T], U8, name="xs", tag="x_scale_bytes", align_bytes=64)
-        xw = [sbuf("xw%d" % g, [P, T], I32) for g in range(PASSES)]
-        HC = H // HALVES
-        wraw = [sbuf("wraw%d" % g, [P, PACK, H], F32) for g in range(PASSES)]
+        offs_t = sbuf("offs_t", [P, S // LIST], U16)
+        pos_t = sbuf("pos_t", [P, V // LIST], U16)
+        neg_t = sbuf("neg_t", [P, U // LIST], U16)
+        e_win = sbuf("e_win", [P, W], I32)
+        e_scale_win = sbuf("e_scale_win", [P, W], U8)
+        x_scale_win = sbuf("x_scale_win", [P, T], U8, tag="x_scale_bytes")
+        x_win = [sbuf("x_win%d" % g, [P, T], I32) for g in range(PASSES)]
+        w_raw = [sbuf("w_raw%d" % g, [P, PACK, H], F32) for g in range(PASSES)]
         gain_t = sbuf("gain_t", [P, V], F32)
 
-        warm_in = sbuf("warm_in", [P, 1], F32)
-        warm_out = sbuf("warm_out", [P, 1], F32)
-        nc.vector.memset(warm_in[:], 0.0)
-        nc.scalar.activation(out=warm_out[:], in_=warm_in[:], func=ACT.Sigmoid)
-
-        nc.gpsimd.memset(es[:].bitcast(I32), 0)
-        nc.vector.memset(xs[:].bitcast(I32), 0)
+        nc.gpsimd.memset(e_scale_win[:].bitcast(I32), 0)
+        nc.vector.memset(x_scale_win[:].bitcast(I32), 0)
 
         def load_w(g):
-            rows = w1[512 * g : 512 * (g + 1), :]
-            nc.sync.dma_start(out=wraw[g][:], in_=rows.rearrange("(p r) c -> p r c", r=PACK))
+            rows = w1[P * PACK * g : P * PACK * (g + 1), :]
+            nc.sync.dma_start(out=w_raw[g][:], in_=rows.rearrange("(p r) c -> p r c", r=PACK))
 
         def load_x(g):
-            nc.sync.dma_start(out=xw[g][:], in_=x_words[g].rearrange("p n t -> p (n t)").bitcast(I32))
+            nc.sync.dma_start(out=x_win[g][:], in_=x_words[g].rearrange("p n t -> p (n t)").bitcast(I32))
 
-        def load_xs(n):
+        def load_x_scales(n):
             r, g = divmod(n, PASSES)
-            nc.sync.dma_start(out=xs[4 * g + r : P : 32, :].bitcast(I32), in_=x_scales[g, r:16:4, :].bitcast(I32))
+            nc.sync.dma_start(
+                out=x_scale_win[4 * g + r : P : QUADRANT, :].bitcast(I32), in_=x_scales[g, r:16:4, :].bitcast(I32)
+            )
 
-        nc.sync.dma_start(out=ew[:], in_=e_words[0].rearrange("p n t -> p (n t)").bitcast(I32))
+        nc.sync.dma_start(out=e_win[:], in_=e_words[0].rearrange("p n t -> p (n t)").bitcast(I32))
         nc.sync.dma_start(neg_t[:], neg)
         nc.sync.dma_start(pos_t[:], pos)
         for r in range(4):
-            nc.sync.dma_start(out=es[E_ROW + r : P : 32, :].bitcast(I32), in_=e_scales[0, r:16:4, :].bitcast(I32))
+            nc.sync.dma_start(
+                out=e_scale_win[E_FIRST + r : P : QUADRANT, :].bitcast(I32), in_=e_scales[0, r:16:4, :].bitcast(I32)
+            )
         load_w(0)
         nc.sync.dma_start(offs_t[:], offs)
-        for n in range(3):
-            load_xs(n)
+        for n in range(XS_AHEAD):
+            load_x_scales(n)
         load_x(0)
-        for n in range(3, 8):
-            load_xs(n)
+        for n in range(XS_AHEAD, 4 * PASSES):
+            load_x_scales(n)
         load_w(1)
         load_x(1)
         nc.sync.dma_start(out=gain_t[:], in_=gain)
 
-        negw_g = sbuf("negw_g", [P, U], U32)
-        negs_g = sbuf("negs_g", [P, U], U8)
-        posw = sbuf("posw", [P, V], U32)
-        poss = sbuf("poss", [P, V], U8)
-        negw = sbuf("negw", [P, U], U32)
-        negs = sbuf("negs", [P, U], U8)
-        nc.vector.tensor_copy(out=negw_g[:], in_=ew[:].bitcast(U32).indirect(neg_t[:]))
-        nc.vector.tensor_copy(out=posw[:], in_=ew[:].bitcast(U32).indirect(pos_t[:]))
-        nc.vector.tensor_copy(out=negs_g[:], in_=es[:].indirect(neg_t[:]))
-        nc.vector.tensor_copy(out=poss[:], in_=es[:].indirect(pos_t[:]))
-        nc.vector.tensor_copy(
-            out=negw[:].rearrange("p (d v) -> p v d", d=2), in_=negw_g[:].rearrange("p (v d) -> p v d", d=2)
-        )
-        nc.vector.tensor_copy(
-            out=negs[:].rearrange("p (d v) -> p v d", d=2), in_=negs_g[:].rearrange("p (v d) -> p v d", d=2)
-        )
+        neg_words_listed = sbuf("neg_words_listed", [P, U], U32)
+        neg_scales_listed = sbuf("neg_scales_listed", [P, U], U8)
+        pos_words = sbuf("pos_words", [P, V], U32)
+        pos_scales = sbuf("pos_scales", [P, V], U8)
+        neg_words = sbuf("neg_words", [P, U], U32)
+        neg_scales = sbuf("neg_scales", [P, U], U8)
+        nc.vector.tensor_copy(out=neg_words_listed[:], in_=e_win[:].bitcast(U32).indirect(neg_t[:]))
+        nc.vector.tensor_copy(out=pos_words[:], in_=e_win[:].bitcast(U32).indirect(pos_t[:]))
+        nc.vector.tensor_copy(out=neg_scales_listed[:], in_=e_scale_win[:].indirect(neg_t[:]))
+        nc.vector.tensor_copy(out=pos_scales[:], in_=e_scale_win[:].indirect(pos_t[:]))
+        for dealt, listed in ((neg_words, neg_words_listed), (neg_scales, neg_scales_listed)):
+            nc.vector.tensor_copy(
+                out=dealt[:].rearrange("p (d v) -> p v d", d=D), in_=listed[:].rearrange("p (v d) -> p v d", d=D)
+            )
 
-        wb = [sbuf("wb%d" % g, [P, PACK, P, PACK], BF16) for g in range(PASSES)]
-        wq = [sbuf("wq%d" % g, [P, H], U32) for g in range(PASSES)]
-        wsc = [sbuf("wsc%d" % g, [P, H], U8) for g in range(PASSES)]
+        w_bf = [sbuf("w_bf%d" % g, [P, PACK, P, PACK], BF16) for g in range(PASSES)]
+        w_words = [sbuf("w_words%d" % g, [P, H], U32) for g in range(PASSES)]
+        w_scales = [sbuf("w_scales%d" % g, [P, H], U8) for g in range(PASSES)]
 
-        def cast_w(copy, g, a):
+        def cast_by_activation(out, in_):
+            nc.scalar.activation(out=out, in_=in_, func=ACT.Copy)
+
+        def cast_w(copy, g, half):
             copy(
-                out=wb[g][:, 2 * a : 2 * a + 2, :, :].rearrange("p j m r -> p m r j"),
-                in_=wraw[g][:].rearrange("p r (m j) -> p m r j", j=PACK)[:, :, :, 2 * a : 2 * a + 2],
+                out=w_bf[g][:, 2 * half : 2 * half + 2, :, :].rearrange("p j m r -> p m r j"),
+                in_=w_raw[g][:].rearrange("p r (m j) -> p m r j", j=PACK)[:, :, :, 2 * half : 2 * half + 2],
             )
 
-        def quant_w(g, a):
+        def quantise_w(g, half):
+            cols = slice(2 * P * half, 2 * P * (half + 1))
             nc.vector.quantize_mx(
-                out=wq[g][:, HC * a : HC * (a + 1)].bitcast(FP8X4),
-                scales=wsc[g][:, HC * a : HC * (a + 1)],
-                in_=wb[g][:, 2 * a : 2 * a + 2, :, :].rearrange("p j m r -> p (j m r)"),
+                out=w_words[g][:, cols].bitcast(FP8X4),
+                scales=w_scales[g][:, cols],
+                in_=w_bf[g][:, 2 * half : 2 * half + 2, :, :].rearrange("p j m r -> p (j m r)"),
             )
 
-        xsg = sbuf("xsg", [P, S], U8)
-        SH = S // 2
-        xg = [
-            [sb.tile([P, SH], U32, name="xg00", tag="x_scale_bytes", align_bytes=64), sbuf("xg01", [P, SH], U32)],
-            [sbuf("xg10", [P, SH], U32), sbuf("xg11", [P, SH], U32)],
+        x_picked_scales = sbuf("x_picked_scales", [P, S], U8)
+        x_picked = [
+            [
+                sbuf("x_picked%d%d" % (g, half), [P, S // 2], U32, tag="x_scale_bytes" if g == half == 0 else None)
+                for half in range(2)
+            ]
+            for g in range(PASSES)
         ]
 
-        def gather_x(g, a):
-            cols = slice(a * SH // 16, (a + 1) * SH // 16)
-            nc.vector.tensor_copy(out=xg[g][a][:], in_=xw[g][:].bitcast(U32).indirect(offs_t[:, cols]))
+        def gather_x(g, half):
+            cols = slice(half * S // 2 // LIST, (half + 1) * S // 2 // LIST)
+            nc.vector.tensor_copy(out=x_picked[g][half][:], in_=x_win[g][:].bitcast(U32).indirect(offs_t[:, cols]))
 
-        hb = [psum.tile([P, PACK, P], F32, name="hb%d" % i, tag="bank%d" % i) for i in range(TILES)]
-        zb = [psum.tile([P, U], F32, name="zb%d" % i) for i in range(TILES)]
+        h_bank = [psum.tile([P, PACK, P], F32, name="h_bank%d" % i, tag="h_bank%d" % i) for i in range(TILES)]
+        first_bank = [psum.tile([P, V], F32, name="first_bank%d" % i) for i in range(TILES)]
 
         def project(g, i):
-            a, b = divmod(i, 2)
+            half, inner = divmod(i, 2)
             for j in range(PACK):
                 nc.tensor.matmul_mx(
-                    out=hb[i][:, j, :],
-                    lhsT=wq[g][:, P * j : P * (j + 1)].bitcast(FP8X4),
-                    lhsT_scale=wsc[g][:, P * j : P * (j + 1)],
-                    rhs=xg[g][a][:, P * b : P * (b + 1)].bitcast(FP8X4),
-                    rhs_scale=xsg[4 * g :, P * i : P * (i + 1)],
+                    out=h_bank[i][:, j, :],
+                    lhsT=w_words[g][:, P * j : P * (j + 1)].bitcast(FP8X4),
+                    lhsT_scale=w_scales[g][:, P * j : P * (j + 1)],
+                    rhs=x_picked[g][half][:, P * inner : P * (inner + 1)].bitcast(FP8X4),
+                    rhs_scale=x_picked_scales[4 * g :, P * i : P * (i + 1)],
                     start=(g == 0 and j == 0),
                     stop=(g == PASSES - 1 and j == PACK - 1),
                 )
 
-        for a in range(HALVES):
-            cast_w(nc.scalar.copy, 0, a)
-            quant_w(0, a)
-        nc.vector.tensor_copy(out=xsg[:], in_=xs[:].indirect(offs_t[:]))
-        gather_x(0, 0)
-        gather_x(0, 1)
+        for half in range(2):
+            cast_w(cast_by_activation, 0, half)
+            quantise_w(0, half)
+        nc.vector.tensor_copy(out=x_picked_scales[:], in_=x_scale_win[:].indirect(offs_t[:]))
+        for half in range(2):
+            gather_x(0, half)
         for i in range(TILES):
             project(0, i)
         cast_w(nc.vector.tensor_copy, 1, 0)
         cast_w(nc.scalar.copy, 1, 1)
-        quant_w(1, 0)
-        quant_w(1, 1)
-        gather_x(1, 0)
-        gather_x(1, 1)
+        for half in range(2):
+            quantise_w(1, half)
+        for half in range(2):
+            gather_x(1, half)
 
-        hb16 = [[sbuf("hb16_%d%d" % (i, sign), [P, H], BF16) for sign in range(2)] for i in range(TILES - 1)]
-        hb16.append([sbuf("hb16_30", [P, H], BF16), sb.tile([P, H], BF16, name="hb16_31", tag="h_last", align_bytes=64)])
-        hq = [[sbuf("hq%d%d" % (i, sign), [P, P], U32) for sign in range(2)] for i in range(TILES)]
-        hs = [[sbuf("hs%d%d" % (i, sign), [P, P], U8) for sign in range(2)] for i in range(TILES)]
-        sg = [sbuf("sg%d" % i, [P, U], F32) for i in range(TILES - 1)]
-        sg.append(sb.tile([P, U], F32, name="sg_last", tag="late", align_bytes=64))
-        rank = sbuf("rank", [P, TILES, V], F32)
+        last = TILES - 1
+        h_bf = [
+            [
+                sbuf("h_bf%d%d" % (i, sign), [P, H], BF16, tag="last_h" if (i, sign) == (last, 1) else None)
+                for sign in range(2)
+            ]
+            for i in range(TILES)
+        ]
+        h_words = [[sbuf("h_words%d%d" % (i, sign), [P, P], U32) for sign in range(2)] for i in range(TILES)]
+        h_scales = [[sbuf("h_scales%d%d" % (i, sign), [P, P], U8) for sign in range(2)] for i in range(TILES)]
+        tanhs = [sbuf("tanhs%d" % i, [P, U], F32, tag="last_tanhs" if i == last else None) for i in range(TILES)]
+        rank2 = sbuf("rank2", [P, TILES, V], F32)
 
-        def drain(i):
-            engine_copy = nc.vector.tensor_copy if i == 1 else nc.scalar.copy
-            engine_copy(out=hb16[i][0][:].rearrange("p (t j) -> p t j", j=PACK), in_=hb[i][:].rearrange("p j t -> p t j"))
+        def empty_h_bank(i):
+            copy = nc.vector.tensor_copy if i == VECTOR_BANK else nc.scalar.copy
+            copy(out=h_bf[i][0][:].rearrange("p (t j) -> p t j", j=PACK), in_=h_bank[i][:].rearrange("p j t -> p t j"))
 
-        def negate(i):
-            nc.vector.tensor_scalar(
-                out=hb16[i][1][:], in0=hb16[i][0][:], scalar1=-1.0, scalar2=None, op0=ALU.mult
-            )
+        def quantise_h(i):
+            nc.vector.tensor_scalar(out=h_bf[i][1][:], in0=h_bf[i][0][:], scalar1=-1.0, scalar2=None, op0=ALU.mult)
+            for sign in range(2):
+                nc.vector.quantize_mx(
+                    out=h_words[i][sign][:].bitcast(FP8X4), scales=h_scales[i][sign][:], in_=h_bf[i][sign][:]
+                )
 
-        def quant_h(i, sign):
-            nc.vector.quantize_mx(
-                out=hq[i][sign][:].bitcast(FP8X4), scales=hs[i][sign][:], in_=hb16[i][sign][:]
-            )
-
-        def score_halves(i, spare):
-            banks = [zb[i][:, 0:V], psum.tile([P, V], F32, name="z_second%d" % i, tag=spare)[:]]
-            for d in range(2):
+        def score(i):
+            banks = [first_bank[i], psum.tile([P, V], F32, name="second_bank%d" % i, tag="h_bank%d" % i)]
+            for d in range(D):
+                cols = slice(V * d, V * (d + 1))
                 nc.tensor.matmul_mx(
-                    out=banks[d], lhsT=hq[i][0][:].bitcast(FP8X4), lhsT_scale=hs[i][0][:],
-                    rhs=negw[:, V * d : V * (d + 1)].bitcast(FP8X4), rhs_scale=negs[E_ROW:, V * d : V * (d + 1)],
-                    start=True, stop=False,
+                    out=banks[d][:], lhsT=h_words[i][0][:].bitcast(FP8X4), lhsT_scale=h_scales[i][0][:],
+                    rhs=neg_words[:, cols].bitcast(FP8X4), rhs_scale=neg_scales[E_FIRST:, cols], start=True, stop=False,
                 )
                 nc.tensor.matmul_mx(
-                    out=banks[d], lhsT=hq[i][1][:].bitcast(FP8X4), lhsT_scale=hs[i][1][:],
-                    rhs=posw[:].bitcast(FP8X4), rhs_scale=poss[E_ROW:, :], start=False, stop=True,
+                    out=banks[d][:], lhsT=h_words[i][1][:].bitcast(FP8X4), lhsT_scale=h_scales[i][1][:],
+                    rhs=pos_words[:].bitcast(FP8X4), rhs_scale=pos_scales[E_FIRST:, :], start=False, stop=True,
                 )
-                nc.scalar.activation(out=sg[i][:, V * d : V * (d + 1)], in_=banks[d], func=ACT.Sigmoid, scale=4.0)
+                nc.scalar.activation(out=tanhs[i][:, cols], in_=banks[d][:], func=ACT.Tanh, scale=2.0)
 
         def add_up(i):
             nc.vector.scalar_tensor_tensor(
-                out=rank[:, i, :], in0=sg[i][:, 0:V], scalar=1.0, in1=sg[i][:, V : 2 * V], op0=ALU.add, op1=ALU.add
+                out=rank2[:, i, :], in0=tanhs[i][:, 0:V], scalar=4.0, in1=tanhs[i][:, V:U], op0=ALU.add, op1=ALU.add
             )
 
         for i in range(TILES):
             project(1, i)
-            drain(i)
+            empty_h_bank(i)
         for i in range(TILES):
-            negate(i)
-            quant_h(i, 0)
-            quant_h(i, 1)
-            score_halves(i, "bank%d" % i)
-        RW = V
-        inv = sb.tile([P, RW], F32, name="inv", tag="h_last", align_bytes=64)
-        add_up(0)
-        nc.vector.reciprocal(out=inv[:, 0 : RW // 2], in_=rank[:, 0, 0 : RW // 2])
-        for i in range(1, TILES):
-            add_up(i)
-        nc.vector.reciprocal(out=inv[:, RW // 2 : RW], in_=rank[:, 0, RW // 2 : RW])
+            quantise_h(i)
+            score(i)
 
-        root = sb.tile([P, TILES, V], F32, name="root", tag="late", align_bytes=64)
-        part = sbuf("part", [P, TILES, V], F32)
-        res = sbuf("res", [P, TILES, V], F32)
+        lo, hi = slice(0, V // 2), slice(V // 2, V)
+        pair = sbuf("pair", [P, V // 2], F32, tag="last_h")
+        pair_inv = sbuf("pair_inv", [P, V // 2], F32)
+        cofactor = sbuf("cofactor", [P, 2, V // 2], F32)
+        single_inv = sbuf("single_inv", [P, RECIP_COLS], F32)
+        result = sbuf("result", [P, TILES, V], F32)
 
         def times(dst, a, b):
             nc.vector.tensor_tensor(out=dst, in0=a, in1=b, op=ALU.mult)
 
-        def store(i, cols=slice(0, V)):
-            nc.sync.dma_start(out=out[P * i : P * (i + 1), cols], in_=res[:, i, cols])
+        def twice_times(dst, a, b):
+            nc.vector.scalar_tensor_tensor(out=dst, in0=a, scalar=2.0, in1=b, op0=ALU.mult, op1=ALU.mult)
 
+        def store(i):
+            nc.sync.dma_start(out=out[P * i : P * (i + 1), :], in_=result[:, i, :])
+
+        add_up(0)
+        times(pair[:], rank2[:, 0, lo], rank2[:, 0, hi])
+        twice_times(cofactor[:, 0, :], rank2[:, 0, hi], gain_t[:, lo])
+        twice_times(cofactor[:, 1, :], rank2[:, 0, lo], gain_t[:, hi])
+        nc.vector.reciprocal(out=pair_inv[:], in_=pair[:])
         for i in range(1, TILES):
-            nc.scalar.activation(out=root[:, i, :], in_=rank[:, i, :], func=ACT.Abs_reciprocal_sqrt)
-        times(part[:, 1, :], root[:, 1, :], gain_t[:])
-        times(res[:, 0, :], inv[:], gain_t[:])
+            add_up(i)
+        times(
+            result[:, 0, :].rearrange("p (c v) -> p c v", c=2),
+            cofactor[:],
+            pair_inv[:].unsqueeze(1).to_broadcast([P, 2, V // 2]),
+        )
         store(0)
-        times(res[:, 1, :], part[:, 1, :], root[:, 1, :])
+        nc.vector.reciprocal(out=single_inv[:], in_=rank2[:, 1, 0:RECIP_COLS])
+
+        root = sbuf("root", [P, TILES - 1, V], F32, tag="last_tanhs")
+        part = sbuf("part", [P, TILES - 1, V], F32)
+        rest = slice(RECIP_COLS, V)
+        for i in range(1, TILES):
+            cols = rest if i == 1 else slice(0, V)
+            nc.scalar.activation(
+                out=root[:, i - 1, cols], in_=rank2[:, i, cols], func=ACT.Abs_reciprocal_sqrt, scale=0.5
+            )
+        times(part[:, 0, rest], root[:, 0, rest], gain_t[:, rest])
+        twice_times(result[:, 1, 0:RECIP_COLS], single_inv[:], gain_t[:, 0:RECIP_COLS])
+        times(result[:, 1, rest], part[:, 0, rest], root[:, 0, rest])
         store(1)
-        for i, cols in ((2, slice(0, V)), (3, slice(0, V))):
-            nc.scalar.activation(out=part[:, i, cols], in_=root[:, i, cols], func=ACT.Square)
-            times(res[:, i, cols], part[:, i, cols], gain_t[:, cols])
-            store(i, cols)
+        for i in range(2, TILES):
+            nc.scalar.activation(out=part[:, i - 1, :], in_=root[:, i - 1, :], func=ACT.Square)
+            times(result[:, i, :], part[:, i - 1, :], gain_t[:])
+            store(i)

@@ -25,7 +25,7 @@ QUADRANT = 32
 E_FIRST = 8
 XS_AHEAD = 3
 VECTOR_BANK = 1
-RECIP_COLS = 64
+PAIR_COLS = 128
 
 
 def tile_picked_ysmap_gain_p_kernel(
@@ -83,20 +83,21 @@ def tile_picked_ysmap_gain_p_kernel(
         load_x(1)
         nc.sync.dma_start(out=gain_t[:], in_=gain)
 
-        neg_words_listed = sbuf("neg_words_listed", [P, U], U32)
         neg_scales_listed = sbuf("neg_scales_listed", [P, U], U8)
         pos_words = sbuf("pos_words", [P, V], U32)
         pos_scales = sbuf("pos_scales", [P, V], U8)
         neg_words = sbuf("neg_words", [P, U], U32)
         neg_scales = sbuf("neg_scales", [P, U], U8)
-        nc.vector.tensor_copy(out=neg_words_listed[:], in_=e_win[:].bitcast(U32).indirect(neg_t[:]))
+        nc.vector.tensor_copy(
+            out=neg_words[:].rearrange("p (d v) -> p v d", d=D), in_=e_win[:].bitcast(U32).indirect(neg_t[:])
+        )
         nc.vector.tensor_copy(out=pos_words[:], in_=e_win[:].bitcast(U32).indirect(pos_t[:]))
         nc.vector.tensor_copy(out=neg_scales_listed[:], in_=e_scale_win[:].indirect(neg_t[:]))
         nc.vector.tensor_copy(out=pos_scales[:], in_=e_scale_win[:].indirect(pos_t[:]))
-        for dealt, listed in ((neg_words, neg_words_listed), (neg_scales, neg_scales_listed)):
-            nc.vector.tensor_copy(
-                out=dealt[:].rearrange("p (d v) -> p v d", d=D), in_=listed[:].rearrange("p (v d) -> p v d", d=D)
-            )
+        nc.vector.tensor_copy(
+            out=neg_scales[:].rearrange("p (d v) -> p v d", d=D),
+            in_=neg_scales_listed[:].rearrange("p (v d) -> p v d", d=D),
+        )
 
         w_bf = [sbuf("w_bf%d" % g, [P, PACK, P, PACK], BF16) for g in range(PASSES)]
         w_words = [sbuf("w_words%d" % g, [P, H], U32) for g in range(PASSES)]
@@ -213,11 +214,12 @@ def tile_picked_ysmap_gain_p_kernel(
             quantise_h(i)
             score(i)
 
-        lo, hi = slice(0, V // 2), slice(V // 2, V)
-        pair = sbuf("pair", [P, V // 2], F32, tag="last_h")
-        pair_inv = sbuf("pair_inv", [P, V // 2], F32)
-        cofactor = sbuf("cofactor", [P, 2, V // 2], F32)
-        single_inv = sbuf("single_inv", [P, RECIP_COLS], F32)
+        half_cols = PAIR_COLS // 2
+        lo, hi, rest = slice(0, half_cols), slice(half_cols, PAIR_COLS), slice(PAIR_COLS, V)
+        pair = sbuf("pair", [P, half_cols], F32, tag="last_h")
+        pair_inv = sbuf("pair_inv", [P, half_cols], F32)
+        cofactor = sbuf("cofactor", [P, 2, half_cols], F32)
+        squared = sbuf("squared", [P, TILES, V], F32)
         result = sbuf("result", [P, TILES, V], F32)
 
         def times(dst, a, b):
@@ -229,34 +231,30 @@ def tile_picked_ysmap_gain_p_kernel(
         def store(i):
             nc.sync.dma_start(out=out[P * i : P * (i + 1), :], in_=result[:, i, :])
 
+        def columns(i):
+            return rest if i == 0 else slice(0, V)
+
         add_up(0)
         times(pair[:], rank2[:, 0, lo], rank2[:, 0, hi])
         twice_times(cofactor[:, 0, :], rank2[:, 0, hi], gain_t[:, lo])
         twice_times(cofactor[:, 1, :], rank2[:, 0, lo], gain_t[:, hi])
-        nc.vector.reciprocal(out=pair_inv[:], in_=pair[:])
+        times(squared[:, 0, rest], rank2[:, 0, rest], rank2[:, 0, rest])
         for i in range(1, TILES):
             add_up(i)
+            if i == 1:
+                nc.vector.reciprocal(out=pair_inv[:], in_=pair[:])
+            times(squared[:, i, :], rank2[:, i, :], rank2[:, i, :])
         times(
-            result[:, 0, :].rearrange("p (c v) -> p c v", c=2),
+            result[:, 0, 0:PAIR_COLS].rearrange("p (c v) -> p c v", c=2),
             cofactor[:],
-            pair_inv[:].unsqueeze(1).to_broadcast([P, 2, V // 2]),
+            pair_inv[:].unsqueeze(1).to_broadcast([P, 2, half_cols]),
         )
-        store(0)
-        nc.vector.reciprocal(out=single_inv[:], in_=rank2[:, 1, 0:RECIP_COLS])
 
-        root = sbuf("root", [P, TILES - 1, V], F32, tag="last_tanhs")
-        part = sbuf("part", [P, TILES - 1, V], F32)
-        rest = slice(RECIP_COLS, V)
-        for i in range(1, TILES):
-            cols = rest if i == 1 else slice(0, V)
+        inverse = sbuf("inverse", [P, TILES, V], F32, tag="last_tanhs")
+        for i in range(TILES):
+            cols = columns(i)
             nc.scalar.activation(
-                out=root[:, i - 1, cols], in_=rank2[:, i, cols], func=ACT.Abs_reciprocal_sqrt, scale=0.5
+                out=inverse[:, i, cols], in_=squared[:, i, cols], func=ACT.Abs_reciprocal_sqrt, scale=0.25
             )
-        times(part[:, 0, rest], root[:, 0, rest], gain_t[:, rest])
-        twice_times(result[:, 1, 0:RECIP_COLS], single_inv[:], gain_t[:, 0:RECIP_COLS])
-        times(result[:, 1, rest], part[:, 0, rest], root[:, 0, rest])
-        store(1)
-        for i in range(2, TILES):
-            nc.scalar.activation(out=part[:, i - 1, :], in_=root[:, i - 1, :], func=ACT.Square)
-            times(result[:, i, :], part[:, i - 1, :], gain_t[:])
+            times(result[:, i, cols], inverse[:, i, cols], gain_t[:, cols])
             store(i)

@@ -83,21 +83,20 @@ def tile_picked_ysmap_gain_p_kernel(
         load_x(1)
         nc.sync.dma_start(out=gain_t[:], in_=gain)
 
+        neg_words_listed = sbuf("neg_words_listed", [P, U], U32)
         neg_scales_listed = sbuf("neg_scales_listed", [P, U], U8)
         pos_words = sbuf("pos_words", [P, V], U32)
         pos_scales = sbuf("pos_scales", [P, V], U8)
         neg_words = sbuf("neg_words", [P, U], U32)
         neg_scales = sbuf("neg_scales", [P, U], U8)
-        nc.vector.tensor_copy(
-            out=neg_words[:].rearrange("p (d v) -> p v d", d=D), in_=e_win[:].bitcast(U32).indirect(neg_t[:])
-        )
+        nc.vector.tensor_copy(out=neg_words_listed[:], in_=e_win[:].bitcast(U32).indirect(neg_t[:]))
         nc.vector.tensor_copy(out=pos_words[:], in_=e_win[:].bitcast(U32).indirect(pos_t[:]))
         nc.vector.tensor_copy(out=neg_scales_listed[:], in_=e_scale_win[:].indirect(neg_t[:]))
         nc.vector.tensor_copy(out=pos_scales[:], in_=e_scale_win[:].indirect(pos_t[:]))
-        nc.vector.tensor_copy(
-            out=neg_scales[:].rearrange("p (d v) -> p v d", d=D),
-            in_=neg_scales_listed[:].rearrange("p (v d) -> p v d", d=D),
-        )
+        for dealt, listed in ((neg_words, neg_words_listed), (neg_scales, neg_scales_listed)):
+            nc.vector.tensor_copy(
+                out=dealt[:].rearrange("p (d v) -> p v d", d=D), in_=listed[:].rearrange("p (v d) -> p v d", d=D)
+            )
 
         w_bf = [sbuf("w_bf%d" % g, [P, PACK, P, PACK], BF16) for g in range(PASSES)]
         w_words = [sbuf("w_words%d" % g, [P, H], U32) for g in range(PASSES)]

@@ -24,8 +24,8 @@ LIST = 16
 QUADRANT = 32
 E_FIRST = 8
 XS_AHEAD = 3
-VECTOR_BANK = 1
-PAIR_COLS = 128
+VECTOR_BANK = 0
+PAIR_COLS = 192
 
 
 def tile_picked_ysmap_gain_p_kernel(
@@ -177,10 +177,39 @@ def tile_picked_ysmap_gain_p_kernel(
         rank2 = sbuf("rank2", [P, TILES, V], F32)
 
         def empty_h_bank(i):
-            copy = nc.vector.tensor_copy if i == VECTOR_BANK else nc.scalar.copy
-            copy(out=h_bf[i][0][:].rearrange("p (t j) -> p t j", j=PACK), in_=h_bank[i][:].rearrange("p j t -> p t j"))
+            dst, src = h_bf[i][0][:].rearrange("p (t j) -> p t j", j=PACK), h_bank[i][:].rearrange("p j t -> p t j")
+            if i == VECTOR_BANK:
+                for half in range(2):
+                    part = slice(half * P // 2, (half + 1) * P // 2)
+                    nc.vector.tensor_copy(out=dst[:, part, :], in_=src[:, part, :])
+            else:
+                nc.scalar.copy(out=dst, in_=src)
+
+        def quantise_first():
+            def negate(half):
+                cols = slice(half * H // 2, (half + 1) * H // 2)
+                nc.vector.tensor_scalar(
+                    out=h_bf[0][1][:, cols], in0=h_bf[0][0][:, cols], scalar1=-1.0, scalar2=None, op0=ALU.mult
+                )
+
+            def codes(sign, half):
+                cols = slice(half * P // 2, (half + 1) * P // 2)
+                nc.vector.quantize_mx(
+                    out=h_words[0][sign][:, cols].bitcast(FP8X4),
+                    scales=h_scales[0][sign][:, cols],
+                    in_=h_bf[0][sign][:, half * H // 2 : (half + 1) * H // 2],
+                )
+
+            negate(0)
+            codes(0, 0)
+            negate(1)
+            codes(1, 0)
+            codes(0, 1)
+            codes(1, 1)
 
         def quantise_h(i):
+            if i == 0:
+                return quantise_first()
             nc.vector.tensor_scalar(out=h_bf[i][1][:], in0=h_bf[i][0][:], scalar1=-1.0, scalar2=None, op0=ALU.mult)
             for sign in range(2):
                 nc.vector.quantize_mx(

@@ -25,7 +25,6 @@ QUADRANT = 32
 E_FIRST = 8
 XS_AHEAD = 3
 VECTOR_BANK = 0
-PAIR_COLS = 192
 
 
 def tile_picked_ysmap_gain_p_kernel(
@@ -242,8 +241,8 @@ def tile_picked_ysmap_gain_p_kernel(
             quantise_h(i)
             score(i)
 
-        half_cols = PAIR_COLS // 2
-        lo, hi, rest = slice(0, half_cols), slice(half_cols, PAIR_COLS), slice(PAIR_COLS, V)
+        half_cols = V // 2
+        lo, hi = slice(0, half_cols), slice(half_cols, V)
         pair = sbuf("pair", [P, half_cols], F32, tag="last_h")
         pair_inv = sbuf("pair_inv", [P, half_cols], F32)
         cofactor = sbuf("cofactor", [P, 2, half_cols], F32)
@@ -259,30 +258,29 @@ def tile_picked_ysmap_gain_p_kernel(
         def store(i):
             nc.sync.dma_start(out=out[P * i : P * (i + 1), :], in_=result[:, i, :])
 
-        def columns(i):
-            return rest if i == 0 else slice(0, V)
+        def halves(ap):
+            return ap.rearrange("p (c v) -> p c v", c=2)
 
         add_up(0)
+        add_up(1)
         times(pair[:], rank2[:, 0, lo], rank2[:, 0, hi])
-        twice_times(cofactor[:, 0, :], rank2[:, 0, hi], gain_t[:, lo])
-        twice_times(cofactor[:, 1, :], rank2[:, 0, lo], gain_t[:, hi])
-        times(squared[:, 0, rest], rank2[:, 0, rest], rank2[:, 0, rest])
+        twice_times(cofactor[:], halves(rank2[:, 0, :])[:, ::-1, :], halves(gain_t[:]))
+        nc.vector.reciprocal(out=pair_inv[:], in_=pair[:])
+        add_up(2)
+        add_up(3)
         for i in range(1, TILES):
-            add_up(i)
-            if i == 1:
-                nc.vector.reciprocal(out=pair_inv[:], in_=pair[:])
             times(squared[:, i, :], rank2[:, i, :], rank2[:, i, :])
         times(
-            result[:, 0, 0:PAIR_COLS].rearrange("p (c v) -> p c v", c=2),
+            result[:, 0, :].rearrange("p (c v) -> p c v", c=2),
             cofactor[:],
             pair_inv[:].unsqueeze(1).to_broadcast([P, 2, half_cols]),
         )
+        store(0)
 
         inverse = sbuf("inverse", [P, TILES, V], F32, tag="last_tanhs")
-        for i in range(TILES):
-            cols = columns(i)
+        for i in range(1, TILES):
             nc.scalar.activation(
-                out=inverse[:, i, cols], in_=squared[:, i, cols], func=ACT.Abs_reciprocal_sqrt, scale=0.25
+                out=inverse[:, i, :], in_=squared[:, i, :], func=ACT.Abs_reciprocal_sqrt, scale=0.25
             )
-            times(result[:, i, cols], inverse[:, i, cols], gain_t[:, cols])
+            times(result[:, i, :], inverse[:, i, :], gain_t[:])
             store(i)

@@ -22,8 +22,8 @@ TILES = S // P
 D = 2
 LIST = 16
 QUADRANT = 32
-E_FIRST = 8
-XS_AHEAD = 3
+BLOCKS = 16
+PLACED_AHEAD = 5
 VECTOR_BANK = 0
 
 
@@ -43,13 +43,14 @@ def tile_picked_ysmap_gain_p_kernel(
         neg_t = sbuf("neg_t", [P, U // LIST], U16)
         e_win = sbuf("e_win", [P, W], I32)
         e_scale_win = sbuf("e_scale_win", [P, W], U8)
-        x_scale_win = sbuf("x_scale_win", [P, T], U8, tag="x_scale_bytes")
+        x_scale_win = sbuf("x_scale_win", [P, T], U8)
         x_win = [sbuf("x_win%d" % g, [P, T], I32) for g in range(PASSES)]
         w_raw = [sbuf("w_raw%d" % g, [P, PACK, H], F32) for g in range(PASSES)]
         gain_t = sbuf("gain_t", [P, V], F32)
 
-        nc.gpsimd.memset(e_scale_win[:].bitcast(I32), 0)
-        nc.vector.memset(x_scale_win[:].bitcast(I32), 0)
+        nc.vector.memset(x_scale_win[:, : T // 2].bitcast(I32), 0)
+        nc.gpsimd.memset(x_scale_win[:, T // 2 :].bitcast(I32), 0)
+        nc.vector.memset(e_scale_win[:].bitcast(I32), 0)
 
         def load_w(g):
             rows = w1[P * PACK * g : P * PACK * (g + 1), :]
@@ -58,44 +59,66 @@ def tile_picked_ysmap_gain_p_kernel(
         def load_x(g):
             nc.sync.dma_start(out=x_win[g][:], in_=x_words[g].rearrange("p n t -> p (n t)").bitcast(I32))
 
-        def load_x_scales(n):
-            r, g = divmod(n, PASSES)
-            nc.sync.dma_start(
-                out=x_scale_win[4 * g + r : P : QUADRANT, :].bitcast(I32), in_=x_scales[g, r:16:4, :].bitcast(I32)
-            )
+        def load_e(cols):
+            nc.sync.dma_start(out=e_win[:, cols], in_=e_words[0].rearrange("p n t -> p (n t)").bitcast(I32)[:, cols])
 
-        nc.sync.dma_start(out=e_win[:], in_=e_words[0].rearrange("p n t -> p (n t)").bitcast(I32))
+        x_step = P // (PASSES * BLOCKS)
+        e_step = P // BLOCKS
+        load_e(slice(0, W // 2))
+        nc.sync.dma_start(offs_t[:], offs)
         nc.sync.dma_start(neg_t[:], neg)
         nc.sync.dma_start(pos_t[:], pos)
-        for r in range(4):
-            nc.sync.dma_start(
-                out=e_scale_win[E_FIRST + r : P : QUADRANT, :].bitcast(I32), in_=e_scales[0, r:16:4, :].bitcast(I32)
-            )
+        nc.sync.dma_start(
+            out=x_scale_win[0:P:x_step, :].bitcast(I32), in_=x_scales.rearrange("g b n -> (g b) n").bitcast(I32)
+        )
+        load_e(slice(W // 2, W))
+        nc.sync.dma_start(out=e_scale_win[0:P:e_step, :].bitcast(I32), in_=e_scales[0].bitcast(I32))
         load_w(0)
-        nc.sync.dma_start(offs_t[:], offs)
-        for n in range(XS_AHEAD):
-            load_x_scales(n)
         load_x(0)
-        for n in range(XS_AHEAD, 4 * PASSES):
-            load_x_scales(n)
+
+        x_scale_rows = sbuf("x_scale_rows", [P, S], U8)
+        x_picked_scales = sbuf("x_picked_scales", [P, S], U8)
+        nc.vector.tensor_copy(out=x_scale_rows[:], in_=x_scale_win[:].indirect(offs_t[:]))
+
+        def place_x(n):
+            g, r = divmod(n, 4)
+            first = x_step * (BLOCKS * g + r)
+            nc.sync.dma_start(
+                out=x_picked_scales[4 * g + r : P : QUADRANT, :].bitcast(I32),
+                in_=x_scale_rows[first : x_step * BLOCKS * (g + 1) : 4 * x_step, :].bitcast(I32),
+            )
+
+        for n in range(PLACED_AHEAD):
+            place_x(n)
         load_w(1)
+        for n in range(PLACED_AHEAD, 4 * PASSES):
+            place_x(n)
         load_x(1)
-        nc.sync.dma_start(out=gain_t[:], in_=gain)
 
         neg_words_listed = sbuf("neg_words_listed", [P, U], U32)
-        neg_scales_listed = sbuf("neg_scales_listed", [P, U], U8)
         pos_words = sbuf("pos_words", [P, V], U32)
-        pos_scales = sbuf("pos_scales", [P, V], U8)
         neg_words = sbuf("neg_words", [P, U], U32)
-        neg_scales = sbuf("neg_scales", [P, U], U8)
         nc.vector.tensor_copy(out=neg_words_listed[:], in_=e_win[:].bitcast(U32).indirect(neg_t[:]))
         nc.vector.tensor_copy(out=pos_words[:], in_=e_win[:].bitcast(U32).indirect(pos_t[:]))
-        nc.vector.tensor_copy(out=neg_scales_listed[:], in_=e_scale_win[:].indirect(neg_t[:]))
-        nc.vector.tensor_copy(out=pos_scales[:], in_=e_scale_win[:].indirect(pos_t[:]))
-        for dealt, listed in ((neg_words, neg_words_listed), (neg_scales, neg_scales_listed)):
-            nc.vector.tensor_copy(
-                out=dealt[:].rearrange("p (d v) -> p v d", d=D), in_=listed[:].rearrange("p (v d) -> p v d", d=D)
+        nc.vector.tensor_copy(
+            out=neg_words[:].rearrange("p (d v) -> p d v", d=D),
+            in_=neg_words_listed[:].rearrange("p (v d) -> p d v", d=D),
+        )
+        e_scales_listed = sbuf("e_scales_listed", [P, U + V], U8)
+        e_scale_rows = sbuf("e_scale_rows", [P, U + V], U8)
+        e_plane = sbuf("e_plane", [P, U + V], U8)
+        nc.vector.tensor_copy(out=e_scales_listed[:, :U], in_=e_scale_win[:].indirect(neg_t[:]))
+        nc.vector.tensor_copy(out=e_scales_listed[:, U:], in_=e_scale_win[:].indirect(pos_t[:]))
+        nc.vector.tensor_copy(
+            out=e_scale_rows[:, :U].rearrange("p (d v) -> p v d", d=D),
+            in_=e_scales_listed[:, :U].rearrange("p (v d) -> p v d", d=D),
+        )
+        nc.vector.tensor_copy(out=e_scale_rows[:, U:].bitcast(I32), in_=e_scales_listed[:, U:].bitcast(I32))
+        for r in range(4):
+            nc.sync.dma_start(
+                out=e_plane[r:P:QUADRANT, :].bitcast(I32), in_=e_scale_rows[e_step * r : P : 4 * e_step, :].bitcast(I32)
             )
+        nc.sync.dma_start(out=gain_t[:], in_=gain)
 
         w_bf = [sbuf("w_bf%d" % g, [P, PACK, P, PACK], BF16) for g in range(PASSES)]
         w_words = [sbuf("w_words%d" % g, [P, H], U32) for g in range(PASSES)]
@@ -118,14 +141,7 @@ def tile_picked_ysmap_gain_p_kernel(
                 in_=w_bf[g][:, 2 * half : 2 * half + 2, :, :].rearrange("p j m r -> p (j m r)"),
             )
 
-        x_picked_scales = sbuf("x_picked_scales", [P, S], U8)
-        x_picked = [
-            [
-                sbuf("x_picked%d%d" % (g, half), [P, S // 2], U32, tag="x_scale_bytes" if g == half == 0 else None)
-                for half in range(2)
-            ]
-            for g in range(PASSES)
-        ]
+        x_picked = [[sbuf("x_picked%d%d" % (g, half), [P, S // 2], U32) for half in range(2)] for g in range(PASSES)]
 
         def gather_x(g, half):
             cols = slice(half * S // 2 // LIST, (half + 1) * S // 2 // LIST)
@@ -150,7 +166,6 @@ def tile_picked_ysmap_gain_p_kernel(
         for half in range(2):
             cast_w(cast_by_activation, 0, half)
             quantise_w(0, half)
-        nc.vector.tensor_copy(out=x_picked_scales[:], in_=x_scale_win[:].indirect(offs_t[:]))
         for half in range(2):
             gather_x(0, half)
         for i in range(TILES):
@@ -221,11 +236,11 @@ def tile_picked_ysmap_gain_p_kernel(
                 cols = slice(V * d, V * (d + 1))
                 nc.tensor.matmul_mx(
                     out=banks[d][:], lhsT=h_words[i][0][:].bitcast(FP8X4), lhsT_scale=h_scales[i][0][:],
-                    rhs=neg_words[:, cols].bitcast(FP8X4), rhs_scale=neg_scales[E_FIRST:, cols], start=True, stop=False,
+                    rhs=neg_words[:, cols].bitcast(FP8X4), rhs_scale=e_plane[:, cols], start=True, stop=False,
                 )
                 nc.tensor.matmul_mx(
                     out=banks[d][:], lhsT=h_words[i][1][:].bitcast(FP8X4), lhsT_scale=h_scales[i][1][:],
-                    rhs=pos_words[:].bitcast(FP8X4), rhs_scale=pos_scales[E_FIRST:, :], start=False, stop=True,
+                    rhs=pos_words[:].bitcast(FP8X4), rhs_scale=e_plane[:, U:], start=False, stop=True,
                 )
                 nc.scalar.activation(out=tanhs[i][:, cols], in_=banks[d][:], func=ACT.Tanh, scale=2.0)
 

@@ -23,7 +23,6 @@ D = 2
 LIST = 16
 QUADRANT = 32
 BLOCKS = 16
-PLACED_AHEAD = 5
 VECTOR_BANK = 0
 
 
@@ -77,33 +76,27 @@ def tile_picked_ysmap_gain_p_kernel(
         load_x(0)
 
         x_scale_rows = sbuf("x_scale_rows", [P, S], U8)
-        x_picked_scales = sbuf("x_picked_scales", [P, S], U8)
+        x_planes = [sbuf("x_plane%d" % g, [P, S], U8) for g in range(PASSES)]
         nc.vector.tensor_copy(out=x_scale_rows[:], in_=x_scale_win[:].indirect(offs_t[:]))
 
-        def place_x(n):
-            g, r = divmod(n, 4)
-            first = x_step * (BLOCKS * g + r)
-            nc.sync.dma_start(
-                out=x_picked_scales[4 * g + r : P : QUADRANT, :].bitcast(I32),
-                in_=x_scale_rows[first : x_step * BLOCKS * (g + 1) : 4 * x_step, :].bitcast(I32),
-            )
+        def place_x(g, rows):
+            for r in rows:
+                first = x_step * (BLOCKS * g + r)
+                nc.sync.dma_start(
+                    out=x_planes[g][r:P:QUADRANT, :].bitcast(I32),
+                    in_=x_scale_rows[first : x_step * BLOCKS * (g + 1) : 4 * x_step, :].bitcast(I32),
+                )
 
-        for n in range(PLACED_AHEAD):
-            place_x(n)
+        place_x(0, range(4))
+        place_x(1, range(1))
         load_w(1)
-        for n in range(PLACED_AHEAD, 4 * PASSES):
-            place_x(n)
         load_x(1)
+        place_x(1, range(1, 4))
 
         neg_words_listed = sbuf("neg_words_listed", [P, U], U32)
         pos_words = sbuf("pos_words", [P, V], U32)
-        neg_words = sbuf("neg_words", [P, U], U32)
         nc.vector.tensor_copy(out=neg_words_listed[:], in_=e_win[:].bitcast(U32).indirect(neg_t[:]))
         nc.vector.tensor_copy(out=pos_words[:], in_=e_win[:].bitcast(U32).indirect(pos_t[:]))
-        nc.vector.tensor_copy(
-            out=neg_words[:].rearrange("p (d v) -> p d v", d=D),
-            in_=neg_words_listed[:].rearrange("p (v d) -> p d v", d=D),
-        )
         e_scales_listed = sbuf("e_scales_listed", [P, U + V], U8)
         e_scale_rows = sbuf("e_scale_rows", [P, U + V], U8)
         e_plane = sbuf("e_plane", [P, U + V], U8)
@@ -158,7 +151,7 @@ def tile_picked_ysmap_gain_p_kernel(
                     lhsT=w_words[g][:, P * j : P * (j + 1)].bitcast(FP8X4),
                     lhsT_scale=w_scales[g][:, P * j : P * (j + 1)],
                     rhs=x_picked[g][half][:, P * inner : P * (inner + 1)].bitcast(FP8X4),
-                    rhs_scale=x_picked_scales[4 * g :, P * i : P * (i + 1)],
+                    rhs_scale=x_planes[g][:, P * i : P * (i + 1)],
                     start=(g == 0 and j == 0),
                     stop=(g == PASSES - 1 and j == PACK - 1),
                 )
@@ -176,6 +169,11 @@ def tile_picked_ysmap_gain_p_kernel(
             quantise_w(1, half)
         for half in range(2):
             gather_x(1, half)
+        neg_words = sbuf("neg_words", [P, U], U32, tag="x_scale_rows")
+        nc.vector.tensor_copy(
+            out=neg_words[:].rearrange("p (d v) -> p d v", d=D),
+            in_=neg_words_listed[:].rearrange("p (v d) -> p d v", d=D),
+        )
 
         last = TILES - 1
         h_bf = [

@@ -87,9 +87,10 @@ def tile_picked_ysmap_gain_p_kernel(
                     in_=x_scale_rows[first : x_step * BLOCKS * (g + 1) : 4 * x_step, :].bitcast(I32),
                 )
 
-        place_x(0, range(4))
+        place_x(0, range(3))
         place_x(1, range(1))
         load_w(1)
+        place_x(0, range(3, 4))
         load_x(1)
         place_x(1, range(1, 4))
 

@@ -258,6 +258,8 @@ def tile_picked_ysmap_gain_p_kernel(
         half_cols = V // 2
         lo, hi = slice(0, half_cols), slice(half_cols, V)
         pair = sbuf("pair", [P, half_cols], F32, tag="last_h")
+        quad = sbuf("quad", [P, half_cols // 2], F32)
+        quad_inv = sbuf("quad_inv", [P, half_cols // 2], F32)
         pair_inv = sbuf("pair_inv", [P, half_cols], F32)
         cofactor = sbuf("cofactor", [P, 2, half_cols], F32)
         squared = sbuf("squared", [P, TILES, V], F32)
@@ -279,16 +281,15 @@ def tile_picked_ysmap_gain_p_kernel(
         add_up(1)
         times(pair[:], rank2[:, 0, lo], rank2[:, 0, hi])
         twice_times(cofactor[:], halves(rank2[:, 0, :])[:, ::-1, :], halves(gain_t[:]))
-        nc.vector.reciprocal(out=pair_inv[:], in_=pair[:])
+        times(quad[:], pair[:, : half_cols // 2], pair[:, half_cols // 2 :])
         add_up(2)
+        nc.vector.reciprocal(out=quad_inv[:], in_=quad[:])
+        times(squared[:, 1, :], rank2[:, 1, :], rank2[:, 1, :])
         add_up(3)
-        for i in range(1, TILES):
-            times(squared[:, i, :], rank2[:, i, :], rank2[:, i, :])
-        times(
-            result[:, 0, :].rearrange("p (c v) -> p c v", c=2),
-            cofactor[:],
-            pair_inv[:].unsqueeze(1).to_broadcast([P, 2, half_cols]),
-        )
+        times(squared[:, 2, :], rank2[:, 2, :], rank2[:, 2, :])
+        times(halves(pair_inv[:]), halves(pair[:])[:, ::-1, :], quad_inv[:].unsqueeze(1).to_broadcast([P, 2, half_cols // 2]))
+        times(squared[:, 3, :], rank2[:, 3, :], rank2[:, 3, :])
+        times(halves(result[:, 0, :]), cofactor[:], pair_inv[:].unsqueeze(1).to_broadcast([P, 2, half_cols]))
         store(0)
 
         inverse = sbuf("inverse", [P, TILES, V], F32, tag="last_tanhs")

@@ -21,9 +21,9 @@ PASSES = K // (P * PACK)
 TILES = S // P
 D = 2
 LIST = 16
-QUADRANT = 32
 BLOCKS = 16
-VECTOR_BANK = 0
+QUADRANT = 32
+ROWS = 4
 
 
 def tile_picked_ysmap_gain_p_kernel(
@@ -36,6 +36,9 @@ def tile_picked_ysmap_gain_p_kernel(
 
         def sbuf(name, shape, dtype, tag=None):
             return sb.tile(shape, dtype, name=name, tag=tag or name, align_bytes=64)
+
+        def halves(ap):
+            return ap.rearrange("p (c v) -> p c v", c=2)
 
         offs_t = sbuf("offs_t", [P, S // LIST], U16)
         pos_t = sbuf("pos_t", [P, V // LIST], U16)
@@ -79,20 +82,21 @@ def tile_picked_ysmap_gain_p_kernel(
         x_planes = [sbuf("x_plane%d" % g, [P, S], U8) for g in range(PASSES)]
         nc.vector.tensor_copy(out=x_scale_rows[:], in_=x_scale_win[:].indirect(offs_t[:]))
 
-        def place_x(g, rows):
-            for r in rows:
-                first = x_step * (BLOCKS * g + r)
-                nc.sync.dma_start(
-                    out=x_planes[g][r:P:QUADRANT, :].bitcast(I32),
-                    in_=x_scale_rows[first : x_step * BLOCKS * (g + 1) : 4 * x_step, :].bitcast(I32),
-                )
+        def place_x(g, r, cols=slice(0, S)):
+            first = x_step * (BLOCKS * g + r)
+            nc.sync.dma_start(
+                out=x_planes[g][r:P:QUADRANT, cols].bitcast(I32),
+                in_=x_scale_rows[first : x_step * BLOCKS * (g + 1) : ROWS * x_step, cols].bitcast(I32),
+            )
 
-        place_x(0, range(3))
-        place_x(1, range(1))
+        for r in range(ROWS - 1):
+            place_x(0, r)
+        place_x(0, ROWS - 1, slice(0, S // 2))
         load_w(1)
-        place_x(0, range(3, 4))
+        place_x(0, ROWS - 1, slice(S // 2, S))
         load_x(1)
-        place_x(1, range(1, 4))
+        for r in range(ROWS):
+            place_x(1, r)
 
         neg_words_listed = sbuf("neg_words_listed", [P, U], U32)
         pos_words = sbuf("pos_words", [P, V], U32)
@@ -108,9 +112,10 @@ def tile_picked_ysmap_gain_p_kernel(
             in_=e_scales_listed[:, :U].rearrange("p (v d) -> p v d", d=D),
         )
         nc.vector.tensor_copy(out=e_scale_rows[:, U:].bitcast(I32), in_=e_scales_listed[:, U:].bitcast(I32))
-        for r in range(4):
+        for r in range(ROWS):
             nc.sync.dma_start(
-                out=e_plane[r:P:QUADRANT, :].bitcast(I32), in_=e_scale_rows[e_step * r : P : 4 * e_step, :].bitcast(I32)
+                out=e_plane[r:P:QUADRANT, :].bitcast(I32),
+                in_=e_scale_rows[e_step * r : P : ROWS * e_step, :].bitcast(I32),
             )
         nc.sync.dma_start(out=gain_t[:], in_=gain)
 
@@ -121,18 +126,18 @@ def tile_picked_ysmap_gain_p_kernel(
         def cast_by_activation(out, in_):
             nc.scalar.activation(out=out, in_=in_, func=ACT.Copy)
 
-        def cast_w(copy, g, half):
+        def cast_w(copy, g, j):
             copy(
-                out=w_bf[g][:, 2 * half : 2 * half + 2, :, :].rearrange("p j m r -> p m r j"),
-                in_=w_raw[g][:].rearrange("p r (m j) -> p m r j", j=PACK)[:, :, :, 2 * half : 2 * half + 2],
+                out=w_bf[g][:, j : j + 2, :, :].rearrange("p j m r -> p m r j"),
+                in_=w_raw[g][:].rearrange("p r (m j) -> p m r j", j=PACK)[:, :, :, j : j + 2],
             )
 
-        def quantise_w(g, half):
-            cols = slice(2 * P * half, 2 * P * (half + 1))
+        def quantise_w(g, j):
+            cols = slice(P * j, P * (j + 2))
             nc.vector.quantize_mx(
                 out=w_words[g][:, cols].bitcast(FP8X4),
                 scales=w_scales[g][:, cols],
-                in_=w_bf[g][:, 2 * half : 2 * half + 2, :, :].rearrange("p j m r -> p (j m r)"),
+                in_=w_bf[g][:, j : j + 2, :, :].rearrange("p j m r -> p (j m r)"),
             )
 
         x_picked = [[sbuf("x_picked%d%d" % (g, half), [P, S // 2], U32) for half in range(2)] for g in range(PASSES)]
@@ -157,17 +162,17 @@ def tile_picked_ysmap_gain_p_kernel(
                     stop=(g == PASSES - 1 and j == PACK - 1),
                 )
 
-        for half in range(2):
-            cast_w(cast_by_activation, 0, half)
-            quantise_w(0, half)
+        for j in (0, 2):
+            cast_w(cast_by_activation, 0, j)
+            quantise_w(0, j)
         for half in range(2):
             gather_x(0, half)
         for i in range(TILES):
             project(0, i)
         cast_w(nc.vector.tensor_copy, 1, 0)
-        cast_w(nc.scalar.copy, 1, 1)
-        for half in range(2):
-            quantise_w(1, half)
+        cast_w(nc.scalar.copy, 1, 2)
+        for j in (0, 2):
+            quantise_w(1, j)
         for half in range(2):
             gather_x(1, half)
         neg_words = sbuf("neg_words", [P, U], U32, tag="x_scale_rows")
@@ -189,45 +194,24 @@ def tile_picked_ysmap_gain_p_kernel(
         tanhs = [sbuf("tanhs%d" % i, [P, U], F32, tag="last_tanhs" if i == last else None) for i in range(TILES)]
         rank2 = sbuf("rank2", [P, TILES, V], F32)
 
-        def empty_h_bank(i):
-            dst, src = h_bf[i][0][:].rearrange("p (t j) -> p t j", j=PACK), h_bank[i][:].rearrange("p j t -> p t j")
-            if i == VECTOR_BANK:
-                for half in range(2):
-                    part = slice(half * P // 2, (half + 1) * P // 2)
-                    nc.vector.tensor_copy(out=dst[:, part, :], in_=src[:, part, :])
-            else:
-                nc.scalar.copy(out=dst, in_=src)
+        def empty_h_bank(i, copy, queries):
+            copy(
+                out=h_bf[i][0][:].rearrange("p (t j) -> p t j", j=PACK)[:, queries, :],
+                in_=h_bank[i][:].rearrange("p j t -> p t j")[:, queries, :],
+            )
 
-        def quantise_first():
-            def negate(half):
-                cols = slice(half * H // 2, (half + 1) * H // 2)
-                nc.vector.tensor_scalar(
-                    out=h_bf[0][1][:, cols], in0=h_bf[0][0][:, cols], scalar1=-1.0, scalar2=None, op0=ALU.mult
-                )
+        def negate_h(i, queries):
+            cols = slice(PACK * queries.start, PACK * queries.stop)
+            nc.vector.tensor_scalar(
+                out=h_bf[i][1][:, cols], in0=h_bf[i][0][:, cols], scalar1=-1.0, scalar2=None, op0=ALU.mult
+            )
 
-            def codes(sign, half):
-                cols = slice(half * P // 2, (half + 1) * P // 2)
-                nc.vector.quantize_mx(
-                    out=h_words[0][sign][:, cols].bitcast(FP8X4),
-                    scales=h_scales[0][sign][:, cols],
-                    in_=h_bf[0][sign][:, half * H // 2 : (half + 1) * H // 2],
-                )
-
-            negate(0)
-            codes(0, 0)
-            negate(1)
-            codes(1, 0)
-            codes(0, 1)
-            codes(1, 1)
-
-        def quantise_h(i):
-            if i == 0:
-                return quantise_first()
-            nc.vector.tensor_scalar(out=h_bf[i][1][:], in0=h_bf[i][0][:], scalar1=-1.0, scalar2=None, op0=ALU.mult)
-            for sign in range(2):
-                nc.vector.quantize_mx(
-                    out=h_words[i][sign][:].bitcast(FP8X4), scales=h_scales[i][sign][:], in_=h_bf[i][sign][:]
-                )
+        def quantise_h(i, sign, queries):
+            nc.vector.quantize_mx(
+                out=h_words[i][sign][:, queries].bitcast(FP8X4),
+                scales=h_scales[i][sign][:, queries],
+                in_=h_bf[i][sign][:, PACK * queries.start : PACK * queries.stop],
+            )
 
         def score(i):
             banks = [first_bank[i], psum.tile([P, V], F32, name="second_bank%d" % i, tag="h_bank%d" % i)]
@@ -243,53 +227,64 @@ def tile_picked_ysmap_gain_p_kernel(
                 )
                 nc.scalar.activation(out=tanhs[i][:, cols], in_=banks[d][:], func=ACT.Tanh, scale=2.0)
 
+        whole, front, back = slice(0, P), slice(0, P // 2), slice(P // 2, P)
+        project(1, 0)
+        empty_h_bank(0, nc.vector.tensor_copy, front)
+        empty_h_bank(0, nc.vector.tensor_copy, back)
+        for i in range(1, TILES):
+            project(1, i)
+            empty_h_bank(i, nc.scalar.copy, whole)
+        negate_h(0, front)
+        quantise_h(0, 0, front)
+        negate_h(0, back)
+        quantise_h(0, 1, front)
+        quantise_h(0, 0, back)
+        quantise_h(0, 1, back)
+        score(0)
+        for i in range(1, TILES):
+            negate_h(i, whole)
+            for sign in range(2):
+                quantise_h(i, sign, whole)
+            score(i)
+
+        def times(dst, a, b):
+            nc.vector.tensor_tensor(out=dst, in0=a, in1=b, op=ALU.mult)
+
         def add_up(i):
             nc.vector.scalar_tensor_tensor(
                 out=rank2[:, i, :], in0=tanhs[i][:, 0:V], scalar=4.0, in1=tanhs[i][:, V:U], op0=ALU.add, op1=ALU.add
             )
 
-        for i in range(TILES):
-            project(1, i)
-            empty_h_bank(i)
-        for i in range(TILES):
-            quantise_h(i)
-            score(i)
-
-        half_cols = V // 2
-        lo, hi = slice(0, half_cols), slice(half_cols, V)
-        pair = sbuf("pair", [P, half_cols], F32, tag="last_h")
-        quad = sbuf("quad", [P, half_cols // 2], F32)
-        quad_inv = sbuf("quad_inv", [P, half_cols // 2], F32)
-        pair_inv = sbuf("pair_inv", [P, half_cols], F32)
-        cofactor = sbuf("cofactor", [P, 2, half_cols], F32)
-        squared = sbuf("squared", [P, TILES, V], F32)
-        result = sbuf("result", [P, TILES, V], F32)
-
-        def times(dst, a, b):
-            nc.vector.tensor_tensor(out=dst, in0=a, in1=b, op=ALU.mult)
-
-        def twice_times(dst, a, b):
-            nc.vector.scalar_tensor_tensor(out=dst, in0=a, scalar=2.0, in1=b, op0=ALU.mult, op1=ALU.mult)
+        def square(i):
+            times(squared[:, i, :], rank2[:, i, :], rank2[:, i, :])
 
         def store(i):
             nc.sync.dma_start(out=out[P * i : P * (i + 1), :], in_=result[:, i, :])
 
-        def halves(ap):
-            return ap.rearrange("p (c v) -> p c v", c=2)
+        pair = sbuf("pair", [P, V // 2], F32, tag="last_h")
+        quad = sbuf("quad", [P, V // 4], F32)
+        quad_inv = sbuf("quad_inv", [P, V // 4], F32)
+        pair_inv = sbuf("pair_inv", [P, V // 2], F32)
+        cofactor = sbuf("cofactor", [P, 2, V // 2], F32)
+        squared = sbuf("squared", [P, TILES, V], F32)
+        result = sbuf("result", [P, TILES, V], F32)
 
         add_up(0)
         add_up(1)
-        times(pair[:], rank2[:, 0, lo], rank2[:, 0, hi])
-        twice_times(cofactor[:], halves(rank2[:, 0, :])[:, ::-1, :], halves(gain_t[:]))
-        times(quad[:], pair[:, : half_cols // 2], pair[:, half_cols // 2 :])
+        times(pair[:], rank2[:, 0, : V // 2], rank2[:, 0, V // 2 :])
+        nc.vector.scalar_tensor_tensor(
+            out=cofactor[:], in0=halves(rank2[:, 0, :])[:, ::-1, :], scalar=2.0, in1=halves(gain_t[:]),
+            op0=ALU.mult, op1=ALU.mult,
+        )
+        times(quad[:], pair[:, : V // 4], pair[:, V // 4 :])
         add_up(2)
         nc.vector.reciprocal(out=quad_inv[:], in_=quad[:])
-        times(squared[:, 1, :], rank2[:, 1, :], rank2[:, 1, :])
+        square(1)
         add_up(3)
-        times(squared[:, 2, :], rank2[:, 2, :], rank2[:, 2, :])
-        times(halves(pair_inv[:]), halves(pair[:])[:, ::-1, :], quad_inv[:].unsqueeze(1).to_broadcast([P, 2, half_cols // 2]))
-        times(squared[:, 3, :], rank2[:, 3, :], rank2[:, 3, :])
-        times(halves(result[:, 0, :]), cofactor[:], pair_inv[:].unsqueeze(1).to_broadcast([P, 2, half_cols]))
+        square(2)
+        times(halves(pair_inv[:]), halves(pair[:])[:, ::-1, :], quad_inv[:].unsqueeze(1).to_broadcast([P, 2, V // 4]))
+        square(3)
+        times(halves(result[:, 0, :]), cofactor[:], pair_inv[:].unsqueeze(1).to_broadcast([P, 2, V // 2]))
         store(0)
 
         inverse = sbuf("inverse", [P, TILES, V], F32, tag="last_tanhs")

@@ -35,7 +35,7 @@ def tile_picked_ysmap_gain_p_kernel(
         psum = ctx.enter_context(tc.psum_pool(name="psum", bufs=1))
 
         def sbuf(name, shape, dtype, tag=None):
-            return sb.tile(shape, dtype, name=name, tag=tag or name, align_bytes=64)
+            return sb.tile(shape, dtype, name=name, tag=tag or name, align_bytes=256)
 
         def halves(ap):
             return ap.rearrange("p (c v) -> p c v", c=2)
@@ -140,17 +140,22 @@ def tile_picked_ysmap_gain_p_kernel(
                 in_=w_bf[g][:, j : j + 2, :, :].rearrange("p j m r -> p (j m r)"),
             )
 
-        x_picked = [[sbuf("x_picked%d%d" % (g, half), [P, S // 2], U32) for half in range(2)] for g in range(PASSES)]
+        pieces = [2, TILES]
+        x_picked = [
+            [sbuf("x_picked%d%d" % (g, n), [P, S // pieces[g]], U32) for n in range(pieces[g])] for g in range(PASSES)
+        ]
 
-        def gather_x(g, half):
-            cols = slice(half * S // 2 // LIST, (half + 1) * S // 2 // LIST)
-            nc.vector.tensor_copy(out=x_picked[g][half][:], in_=x_win[g][:].bitcast(U32).indirect(offs_t[:, cols]))
+        def gather_x(g, n):
+            width = S // pieces[g] // LIST
+            nc.vector.tensor_copy(
+                out=x_picked[g][n][:], in_=x_win[g][:].bitcast(U32).indirect(offs_t[:, n * width : (n + 1) * width])
+            )
 
         h_bank = [psum.tile([P, PACK, P], F32, name="h_bank%d" % i, tag="h_bank%d" % i) for i in range(TILES)]
-        first_bank = [psum.tile([P, V], F32, name="first_bank%d" % i) for i in range(TILES)]
+        score_bank = [psum.tile([P, U], F32, name="score_bank%d" % i) for i in range(TILES)]
 
         def project(g, i):
-            half, inner = divmod(i, 2)
+            half, inner = divmod(i, TILES // pieces[g])
             for j in range(PACK):
                 nc.tensor.matmul_mx(
                     out=h_bank[i][:, j, :],
@@ -173,8 +178,8 @@ def tile_picked_ysmap_gain_p_kernel(
         cast_w(nc.scalar.copy, 1, 2)
         for j in (0, 2):
             quantise_w(1, j)
-        for half in range(2):
-            gather_x(1, half)
+        for n in range(TILES):
+            gather_x(1, n)
         neg_words = sbuf("neg_words", [P, U], U32, tag="x_scale_rows")
         nc.vector.tensor_copy(
             out=neg_words[:].rearrange("p (d v) -> p d v", d=D),
@@ -214,34 +219,23 @@ def tile_picked_ysmap_gain_p_kernel(
             )
 
         def score(i):
-            banks = [first_bank[i], psum.tile([P, V], F32, name="second_bank%d" % i, tag="h_bank%d" % i)]
+            nc.tensor.matmul_mx(
+                out=score_bank[i][:], lhsT=h_words[i][0][:].bitcast(FP8X4), lhsT_scale=h_scales[i][0][:],
+                rhs=neg_words[:].bitcast(FP8X4), rhs_scale=e_plane[:, :U], start=True, stop=False,
+            )
             for d in range(D):
-                cols = slice(V * d, V * (d + 1))
                 nc.tensor.matmul_mx(
-                    out=banks[d][:], lhsT=h_words[i][0][:].bitcast(FP8X4), lhsT_scale=h_scales[i][0][:],
-                    rhs=neg_words[:, cols].bitcast(FP8X4), rhs_scale=e_plane[:, cols], start=True, stop=False,
+                    out=score_bank[i][:, V * d : V * (d + 1)], lhsT=h_words[i][1][:].bitcast(FP8X4),
+                    lhsT_scale=h_scales[i][1][:], rhs=pos_words[:].bitcast(FP8X4), rhs_scale=e_plane[:, U:],
+                    start=False, stop=(d == D - 1),
                 )
-                nc.tensor.matmul_mx(
-                    out=banks[d][:], lhsT=h_words[i][1][:].bitcast(FP8X4), lhsT_scale=h_scales[i][1][:],
-                    rhs=pos_words[:].bitcast(FP8X4), rhs_scale=e_plane[:, U:], start=False, stop=True,
-                )
-                nc.scalar.activation(out=tanhs[i][:, cols], in_=banks[d][:], func=ACT.Tanh, scale=2.0)
+            nc.scalar.activation(out=tanhs[i][:], in_=score_bank[i][:], func=ACT.Tanh, scale=2.0)
 
-        whole, front, back = slice(0, P), slice(0, P // 2), slice(P // 2, P)
-        project(1, 0)
-        empty_h_bank(0, nc.vector.tensor_copy, front)
-        empty_h_bank(0, nc.vector.tensor_copy, back)
-        for i in range(1, TILES):
+        whole = slice(0, P)
+        for i in range(TILES):
             project(1, i)
             empty_h_bank(i, nc.scalar.copy, whole)
-        negate_h(0, front)
-        quantise_h(0, 0, front)
-        negate_h(0, back)
-        quantise_h(0, 1, front)
-        quantise_h(0, 0, back)
-        quantise_h(0, 1, back)
-        score(0)
-        for i in range(1, TILES):
+        for i in range(TILES):
             negate_h(i, whole)
             for sign in range(2):
                 quantise_h(i, sign, whole)

@@ -50,9 +50,9 @@ def tile_picked_ysmap_gain_p_kernel(
         w_raw = [sbuf("w_raw%d" % g, [P, PACK, H], F32) for g in range(PASSES)]
         gain_t = sbuf("gain_t", [P, V], F32)
 
-        nc.vector.memset(x_scale_win[:, : T // 2].bitcast(I32), 0)
-        nc.gpsimd.memset(x_scale_win[:, T // 2 :].bitcast(I32), 0)
         nc.vector.memset(e_scale_win[:].bitcast(I32), 0)
+        nc.vector.memset(x_scale_win[QUADRANT : 2 * QUADRANT, :].bitcast(I32), 0)
+        nc.vector.memset(x_scale_win[2 * QUADRANT :, :].bitcast(I32), 0)
 
         def load_w(g):
             rows = w1[P * PACK * g : P * PACK * (g + 1), :]
@@ -64,16 +64,15 @@ def tile_picked_ysmap_gain_p_kernel(
         def load_e(cols):
             nc.sync.dma_start(out=e_win[:, cols], in_=e_words[0].rearrange("p n t -> p (n t)").bitcast(I32)[:, cols])
 
-        x_step = P // (PASSES * BLOCKS)
+        x_step = 1
         e_step = P // BLOCKS
-        load_e(slice(0, W // 2))
+        nc.sync.dma_start(
+            out=x_scale_win[:QUADRANT, :].bitcast(I32), in_=x_scales.rearrange("g b n -> (g b) n").bitcast(I32)
+        )
         nc.sync.dma_start(offs_t[:], offs)
+        load_e(slice(0, W))
         nc.sync.dma_start(neg_t[:], neg)
         nc.sync.dma_start(pos_t[:], pos)
-        nc.sync.dma_start(
-            out=x_scale_win[0:P:x_step, :].bitcast(I32), in_=x_scales.rearrange("g b n -> (g b) n").bitcast(I32)
-        )
-        load_e(slice(W // 2, W))
         nc.sync.dma_start(out=e_scale_win[0:P:e_step, :].bitcast(I32), in_=e_scales[0].bitcast(I32))
         load_w(0)
         load_x(0)

@@ -251,8 +251,8 @@ def tile_picked_ysmap_gain_p_kernel(
         def square(i):
             times(squared[:, i, :], rank2[:, i, :], rank2[:, i, :])
 
-        def store(i):
-            nc.sync.dma_start(out=out[P * i : P * (i + 1), :], in_=result[:, i, :])
+        def store(i, cols=slice(0, V)):
+            nc.sync.dma_start(out=out[P * i : P * (i + 1), cols], in_=result[:, i, cols])
 
         pair = sbuf("pair", [P, V // 2], F32, tag="last_h")
         quad = sbuf("quad", [P, V // 4], F32)
@@ -281,9 +281,18 @@ def tile_picked_ysmap_gain_p_kernel(
         store(0)
 
         inverse = sbuf("inverse", [P, TILES, V], F32, tag="last_tanhs")
-        for i in range(1, TILES):
+        def finish(i, cols):
             nc.scalar.activation(
-                out=inverse[:, i, :], in_=squared[:, i, :], func=ACT.Abs_reciprocal_sqrt, scale=0.25
+                out=inverse[:, i, cols], in_=squared[:, i, cols], func=ACT.Abs_reciprocal_sqrt, scale=0.25
             )
-            times(result[:, i, :], inverse[:, i, :], gain_t[:])
-            store(i)
+            times(result[:, i, cols], inverse[:, i, cols], gain_t[:, cols])
+
+        front, back = slice(0, V // 2), slice(V // 2, V)
+        finish(1, front)
+        finish(1, back)
+        store(1)
+        finish(2, slice(0, V))
+        store(2)
+        for cols in (front, back):
+            finish(last, cols)
+            store(last, cols)

@@ -51,8 +51,8 @@ def tile_picked_ysmap_gain_p_kernel(
         gain_t = sbuf("gain_t", [P, V], F32)
 
         nc.vector.memset(e_scale_win[:].bitcast(I32), 0)
-        nc.vector.memset(x_scale_win[QUADRANT : 2 * QUADRANT, :].bitcast(I32), 0)
-        nc.vector.memset(x_scale_win[2 * QUADRANT :, :].bitcast(I32), 0)
+        nc.vector.memset(x_scale_win[: 2 * QUADRANT, :].bitcast(I32), 0)
+        nc.vector.memset(x_scale_win[3 * QUADRANT :, :].bitcast(I32), 0)
 
         def load_w(g):
             rows = w1[P * PACK * g : P * PACK * (g + 1), :]
@@ -64,16 +64,16 @@ def tile_picked_ysmap_gain_p_kernel(
         def load_e(cols):
             nc.sync.dma_start(out=e_win[:, cols], in_=e_words[0].rearrange("p n t -> p (n t)").bitcast(I32)[:, cols])
 
-        x_step = 1
-        e_step = P // BLOCKS
+        x_first = 2 * QUADRANT
+        e_first = BLOCKS
         nc.sync.dma_start(
-            out=x_scale_win[:QUADRANT, :].bitcast(I32), in_=x_scales.rearrange("g b n -> (g b) n").bitcast(I32)
+            out=x_scale_win[x_first : x_first + QUADRANT, :].bitcast(I32), in_=x_scales.rearrange("g b n -> (g b) n").bitcast(I32)
         )
         nc.sync.dma_start(offs_t[:], offs)
         load_e(slice(0, W))
         nc.sync.dma_start(neg_t[:], neg)
         nc.sync.dma_start(pos_t[:], pos)
-        nc.sync.dma_start(out=e_scale_win[0:P:e_step, :].bitcast(I32), in_=e_scales[0].bitcast(I32))
+        nc.sync.dma_start(out=e_scale_win[e_first : e_first + BLOCKS, :].bitcast(I32), in_=e_scales[0].bitcast(I32))
         load_w(0)
         load_x(0)
 
@@ -82,10 +82,10 @@ def tile_picked_ysmap_gain_p_kernel(
         nc.vector.tensor_copy(out=x_scale_rows[:], in_=x_scale_win[:].indirect(offs_t[:]))
 
         def place_x(g, r, cols=slice(0, S)):
-            first = x_step * (BLOCKS * g + r)
+            first = x_first + BLOCKS * g
             nc.sync.dma_start(
                 out=x_planes[g][r:P:QUADRANT, cols].bitcast(I32),
-                in_=x_scale_rows[first : x_step * BLOCKS * (g + 1) : ROWS * x_step, cols].bitcast(I32),
+                in_=x_scale_rows[first + r : first + BLOCKS : ROWS, cols].bitcast(I32),
             )
 
         for r in range(ROWS - 1):
@@ -114,7 +114,7 @@ def tile_picked_ysmap_gain_p_kernel(
         for r in range(ROWS):
             nc.sync.dma_start(
                 out=e_plane[r:P:QUADRANT, :].bitcast(I32),
-                in_=e_scale_rows[e_step * r : P : ROWS * e_step, :].bitcast(I32),
+                in_=e_scale_rows[e_first + r : e_first + BLOCKS : ROWS, :].bitcast(I32),
             )
         nc.sync.dma_start(out=gain_t[:], in_=gain)
 

@@ -51,8 +51,8 @@ def tile_picked_ysmap_gain_p_kernel(
         gain_t = sbuf("gain_t", [P, V], F32)
 
         nc.vector.memset(e_scale_win[:].bitcast(I32), 0)
-        nc.vector.memset(x_scale_win[: 2 * QUADRANT, :].bitcast(I32), 0)
-        nc.vector.memset(x_scale_win[3 * QUADRANT :, :].bitcast(I32), 0)
+        nc.vector.memset(x_scale_win[QUADRANT : 2 * QUADRANT, :].bitcast(I32), 0)
+        nc.vector.memset(x_scale_win[2 * QUADRANT :, :].bitcast(I32), 0)
 
         def load_w(g):
             rows = w1[P * PACK * g : P * PACK * (g + 1), :]
@@ -64,8 +64,8 @@ def tile_picked_ysmap_gain_p_kernel(
         def load_e(cols):
             nc.sync.dma_start(out=e_win[:, cols], in_=e_words[0].rearrange("p n t -> p (n t)").bitcast(I32)[:, cols])
 
-        x_first = 2 * QUADRANT
-        e_first = BLOCKS
+        x_first = 0
+        e_first = 2 * QUADRANT + BLOCKS
         nc.sync.dma_start(
             out=x_scale_win[x_first : x_first + QUADRANT, :].bitcast(I32), in_=x_scales.rearrange("g b n -> (g b) n").bitcast(I32)
         )
@@ -88,11 +88,18 @@ def tile_picked_ysmap_gain_p_kernel(
                 in_=x_scale_rows[first + r : first + BLOCKS : ROWS, cols].bitcast(I32),
             )
 
-        for r in range(ROWS - 1):
-            place_x(0, r)
-        place_x(0, ROWS - 1, slice(0, S // 2))
+        def place_quadrant(q, cols=slice(0, S)):
+            nc.sync.dma_start(
+                out=x_planes[0][QUADRANT * q : QUADRANT * q + ROWS, cols].bitcast(I32),
+                in_=x_scale_rows[ROWS * q : ROWS * (q + 1), cols].bitcast(I32),
+            )
+
+        nc.vector.tensor_copy(out=x_planes[0][:ROWS, :].bitcast(I32), in_=x_scale_rows[:ROWS, :].bitcast(I32))
+        place_quadrant(1)
+        place_quadrant(2)
+        place_quadrant(3, slice(0, S // 2))
         load_w(1)
-        place_x(0, ROWS - 1, slice(S // 2, S))
+        place_quadrant(3, slice(S // 2, S))
         load_x(1)
         for r in range(ROWS):
             place_x(1, r)
@@ -116,7 +123,8 @@ def tile_picked_ysmap_gain_p_kernel(
                 out=e_plane[r:P:QUADRANT, :].bitcast(I32),
                 in_=e_scale_rows[e_first + r : e_first + BLOCKS : ROWS, :].bitcast(I32),
             )
-        nc.sync.dma_start(out=gain_t[:], in_=gain)
+        for cols in (slice(0, V // 2), slice(V // 2, V)):
+            nc.sync.dma_start(out=gain_t[:, cols], in_=gain[:, cols])
 
         w_bf = [sbuf("w_bf%d" % g, [P, PACK, P, PACK], BF16) for g in range(PASSES)]
         w_words = [sbuf("w_words%d" % g, [P, H], U32) for g in range(PASSES)]

from contextlib import ExitStack

import concourse.mybir as mybir

K, T, S, H, V, W, U = 1024, 2048, 512, 512, 256, 1024, 512
FLOPS = 2 * K * H * S + 2 * H * S * (U + V)

F32 = mybir.dt.float32
BF16 = mybir.dt.bfloat16
I32 = mybir.dt.int32
U32 = mybir.dt.uint32
U16 = mybir.dt.uint16
U8 = mybir.dt.uint8
FP8X4 = mybir.dt.float8_e4m3fn_x4
ACT = mybir.ActivationFunctionType
ALU = mybir.AluOpType

P = 128
PACK = 4
PASSES = K // (P * PACK)
TILES = S // P
D = 2
LIST = 16
BLOCKS = 16
QUADRANT = 32
ROWS = 4


def tile_picked_ysmap_gain_p_kernel(
    tc, x_words, x_scales, w1, e_words, e_scales, gain, offs, pos, neg, out
):
    nc = tc.nc
    with ExitStack() as ctx:
        sb = ctx.enter_context(tc.tile_pool(name="sb", bufs=1))
        psum = ctx.enter_context(tc.psum_pool(name="psum", bufs=1))

        def sbuf(name, shape, dtype, tag=None):
            return sb.tile(shape, dtype, name=name, tag=tag or name, align_bytes=256)

        def halves(ap):
            return ap.rearrange("p (c v) -> p c v", c=2)

        offs_t = sbuf("offs_t", [P, S // LIST], U16)
        pos_t = sbuf("pos_t", [P, V // LIST], U16)
        neg_t = sbuf("neg_t", [P, U // LIST], U16)
        e_win = sbuf("e_win", [P, W], I32)
        e_scale_win = sbuf("e_scale_win", [P, W], U8)
        x_scale_win = sbuf("x_scale_win", [P, T], U8)
        x_win = [sbuf("x_win%d" % g, [P, T], I32) for g in range(PASSES)]
        w_raw = [sbuf("w_raw%d" % g, [P, PACK, H], F32) for g in range(PASSES)]
        gain_t = sbuf("gain_t", [P, V], F32)

        nc.vector.memset(e_scale_win[:].bitcast(I32), 0)
        nc.vector.memset(x_scale_win[QUADRANT : 2 * QUADRANT, :].bitcast(I32), 0)
        nc.vector.memset(x_scale_win[2 * QUADRANT :, :].bitcast(I32), 0)

        def load_w(g):
            rows = w1[P * PACK * g : P * PACK * (g + 1), :]
            nc.sync.dma_start(out=w_raw[g][:], in_=rows.rearrange("(p r) c -> p r c", r=PACK))

        def load_x(g):
            nc.sync.dma_start(out=x_win[g][:], in_=x_words[g].rearrange("p n t -> p (n t)").bitcast(I32))

        def load_e(cols):
            nc.sync.dma_start(out=e_win[:, cols], in_=e_words[0].rearrange("p n t -> p (n t)").bitcast(I32)[:, cols])

        x_first = 0
        e_first = 2 * QUADRANT + BLOCKS
        nc.sync.dma_start(
            out=x_scale_win[x_first : x_first + QUADRANT, :].bitcast(I32), in_=x_scales.rearrange("g b n -> (g b) n").bitcast(I32)
        )
        nc.sync.dma_start(offs_t[:], offs)
        load_e(slice(0, W))
        nc.sync.dma_start(neg_t[:], neg)
        nc.sync.dma_start(pos_t[:], pos)
        nc.sync.dma_start(out=e_scale_win[e_first : e_first + BLOCKS, :].bitcast(I32), in_=e_scales[0].bitcast(I32))
        load_w(0)
        load_x(0)

        x_scale_rows = sbuf("x_scale_rows", [P, S], U8)
        x_planes = [sbuf("x_plane%d" % g, [P, S], U8) for g in range(PASSES)]
        nc.vector.tensor_copy(out=x_scale_rows[:], in_=x_scale_win[:].indirect(offs_t[:]))

        def place_x(g, r, cols=slice(0, S)):
            first = x_first + BLOCKS * g
            nc.sync.dma_start(
                out=x_planes[g][r:P:QUADRANT, cols].bitcast(I32),
                in_=x_scale_rows[first + r : first + BLOCKS : ROWS, cols].bitcast(I32),
            )

        def place_quadrant(q, cols=slice(0, S)):
            nc.sync.dma_start(
                out=x_planes[0][QUADRANT * q : QUADRANT * q + ROWS, cols].bitcast(I32),
                in_=x_scale_rows[ROWS * q : ROWS * (q + 1), cols].bitcast(I32),
            )

        nc.vector.tensor_copy(out=x_planes[0][:ROWS, :].bitcast(I32), in_=x_scale_rows[:ROWS, :].bitcast(I32))
        place_quadrant(1)
        place_quadrant(2)
        place_quadrant(3, slice(0, S // 2))
        load_w(1)
        place_quadrant(3, slice(S // 2, S))
        load_x(1)
        for r in range(ROWS):
            place_x(1, r)

        neg_words_listed = sbuf("neg_words_listed", [P, U], U32)
        pos_words = sbuf("pos_words", [P, V], U32)
        nc.vector.tensor_copy(out=neg_words_listed[:], in_=e_win[:].bitcast(U32).indirect(neg_t[:]))
        nc.vector.tensor_copy(out=pos_words[:], in_=e_win[:].bitcast(U32).indirect(pos_t[:]))
        e_scales_listed = sbuf("e_scales_listed", [P, U + V], U8)
        e_scale_rows = sbuf("e_scale_rows", [P, U + V], U8)
        e_plane = sbuf("e_plane", [P, U + V], U8)
        nc.vector.tensor_copy(out=e_scales_listed[:, :U], in_=e_scale_win[:].indirect(neg_t[:]))
        nc.vector.tensor_copy(out=e_scales_listed[:, U:], in_=e_scale_win[:].indirect(pos_t[:]))
        nc.vector.tensor_copy(
            out=e_scale_rows[:, :U].rearrange("p (d v) -> p v d", d=D),
            in_=e_scales_listed[:, :U].rearrange("p (v d) -> p v d", d=D),
        )
        nc.vector.tensor_copy(out=e_scale_rows[:, U:].bitcast(I32), in_=e_scales_listed[:, U:].bitcast(I32))
        for r in range(ROWS):
            nc.sync.dma_start(
                out=e_plane[r:P:QUADRANT, :].bitcast(I32),
                in_=e_scale_rows[e_first + r : e_first + BLOCKS : ROWS, :].bitcast(I32),
            )
        for cols in (slice(0, V // 2), slice(V // 2, V)):
            nc.sync.dma_start(out=gain_t[:, cols], in_=gain[:, cols])

        w_bf = [sbuf("w_bf%d" % g, [P, PACK, P, PACK], BF16) for g in range(PASSES)]
        w_words = [sbuf("w_words%d" % g, [P, H], U32) for g in range(PASSES)]
        w_scales = [sbuf("w_scales%d" % g, [P, H], U8) for g in range(PASSES)]

        def cast_by_activation(out, in_):
            nc.scalar.activation(out=out, in_=in_, func=ACT.Copy)

        def cast_w(copy, g, j):
            copy(
                out=w_bf[g][:, j : j + 2, :, :].rearrange("p j m r -> p m r j"),
                in_=w_raw[g][:].rearrange("p r (m j) -> p m r j", j=PACK)[:, :, :, j : j + 2],
            )

        def quantise_w(g, j):
            cols = slice(P * j, P * (j + 2))
            nc.vector.quantize_mx(
                out=w_words[g][:, cols].bitcast(FP8X4),
                scales=w_scales[g][:, cols],
                in_=w_bf[g][:, j : j + 2, :, :].rearrange("p j m r -> p (j m r)"),
            )

        pieces = [2, TILES]
        x_picked = [
            [sbuf("x_picked%d%d" % (g, n), [P, S // pieces[g]], U32) for n in range(pieces[g])] for g in range(PASSES)
        ]

        def gather_x(g, n):
            width = S // pieces[g] // LIST
            nc.vector.tensor_copy(
                out=x_picked[g][n][:], in_=x_win[g][:].bitcast(U32).indirect(offs_t[:, n * width : (n + 1) * width])
            )

        h_bank = [psum.tile([P, PACK, P], F32, name="h_bank%d" % i, tag="h_bank%d" % i) for i in range(TILES)]
        score_bank = [psum.tile([P, U], F32, name="score_bank%d" % i) for i in range(TILES)]

        def project(g, i):
            half, inner = divmod(i, TILES // pieces[g])
            for j in range(PACK):
                nc.tensor.matmul_mx(
                    out=h_bank[i][:, j, :],
                    lhsT=w_words[g][:, P * j : P * (j + 1)].bitcast(FP8X4),
                    lhsT_scale=w_scales[g][:, P * j : P * (j + 1)],
                    rhs=x_picked[g][half][:, P * inner : P * (inner + 1)].bitcast(FP8X4),
                    rhs_scale=x_planes[g][:, P * i : P * (i + 1)],
                    start=(g == 0 and j == 0),
                    stop=(g == PASSES - 1 and j == PACK - 1),
                )

        for j in (0, 2):
            cast_w(cast_by_activation, 0, j)
            quantise_w(0, j)
        for half in range(2):
            gather_x(0, half)
        for i in range(TILES):
            project(0, i)
        cast_w(nc.vector.tensor_copy, 1, 0)
        cast_w(nc.scalar.copy, 1, 2)
        for j in (0, 2):
            quantise_w(1, j)
        for n in range(TILES):
            gather_x(1, n)
        neg_words = sbuf("neg_words", [P, U], U32, tag="x_scale_rows")
        nc.vector.tensor_copy(
            out=neg_words[:].rearrange("p (d v) -> p d v", d=D),
            in_=neg_words_listed[:].rearrange("p (v d) -> p d v", d=D),
        )

        last = TILES - 1
        h_bf = [
            [
                sbuf("h_bf%d%d" % (i, sign), [P, H], BF16, tag="last_h" if (i, sign) == (last, 1) else None)
                for sign in range(2)
            ]
            for i in range(TILES)
        ]
        h_words = [[sbuf("h_words%d%d" % (i, sign), [P, P], U32) for sign in range(2)] for i in range(TILES)]
        h_scales = [[sbuf("h_scales%d%d" % (i, sign), [P, P], U8) for sign in range(2)] for i in range(TILES)]
        tanhs = [sbuf("tanhs%d" % i, [P, U], F32, tag="last_tanhs" if i == last else None) for i in range(TILES)]
        rank2 = sbuf("rank2", [P, TILES, V], F32)

        def empty_h_bank(i, copy, queries):
            copy(
                out=h_bf[i][0][:].rearrange("p (t j) -> p t j", j=PACK)[:, queries, :],
                in_=h_bank[i][:].rearrange("p j t -> p t j")[:, queries, :],
            )

        def negate_h(i, queries):
            cols = slice(PACK * queries.start, PACK * queries.stop)
            nc.vector.tensor_scalar(
                out=h_bf[i][1][:, cols], in0=h_bf[i][0][:, cols], scalar1=-1.0, scalar2=None, op0=ALU.mult
            )

        def quantise_h(i, sign, queries):
            nc.vector.quantize_mx(
                out=h_words[i][sign][:, queries].bitcast(FP8X4),
                scales=h_scales[i][sign][:, queries],
                in_=h_bf[i][sign][:, PACK * queries.start : PACK * queries.stop],
            )

        def score(i):
            nc.tensor.matmul_mx(
                out=score_bank[i][:], lhsT=h_words[i][0][:].bitcast(FP8X4), lhsT_scale=h_scales[i][0][:],
                rhs=neg_words[:].bitcast(FP8X4), rhs_scale=e_plane[:, :U], start=True, stop=False,
            )
            for d in range(D):
                nc.tensor.matmul_mx(
                    out=score_bank[i][:, V * d : V * (d + 1)], lhsT=h_words[i][1][:].bitcast(FP8X4),
                    lhsT_scale=h_scales[i][1][:], rhs=pos_words[:].bitcast(FP8X4), rhs_scale=e_plane[:, U:],
                    start=False, stop=(d == D - 1),
                )
            nc.scalar.activation(out=tanhs[i][:], in_=score_bank[i][:], func=ACT.Tanh, scale=2.0)

        whole = slice(0, P)
        for i in range(TILES):
            project(1, i)
            empty_h_bank(i, nc.scalar.copy, whole)
        for i in range(TILES):
            negate_h(i, whole)
            for sign in range(2):
                quantise_h(i, sign, whole)
            score(i)

        def times(dst, a, b):
            nc.vector.tensor_tensor(out=dst, in0=a, in1=b, op=ALU.mult)

        def add_up(i):
            nc.vector.scalar_tensor_tensor(
                out=rank2[:, i, :], in0=tanhs[i][:, 0:V], scalar=4.0, in1=tanhs[i][:, V:U], op0=ALU.add, op1=ALU.add
            )

        def square(i):
            times(squared[:, i, :], rank2[:, i, :], rank2[:, i, :])

        def store(i, cols=slice(0, V)):
            nc.sync.dma_start(out=out[P * i : P * (i + 1), cols], in_=result[:, i, cols])

        pair = sbuf("pair", [P, V // 2], F32, tag="last_h")
        quad = sbuf("quad", [P, V // 4], F32)
        quad_inv = sbuf("quad_inv", [P, V // 4], F32)
        pair_inv = sbuf("pair_inv", [P, V // 2], F32)
        cofactor = sbuf("cofactor", [P, 2, V // 2], F32)
        squared = sbuf("squared", [P, TILES, V], F32)
        result = sbuf("result", [P, TILES, V], F32)

        add_up(0)
        add_up(1)
        times(pair[:], rank2[:, 0, : V // 2], rank2[:, 0, V // 2 :])
        nc.vector.scalar_tensor_tensor(
            out=cofactor[:], in0=halves(rank2[:, 0, :])[:, ::-1, :], scalar=2.0, in1=halves(gain_t[:]),
            op0=ALU.mult, op1=ALU.mult,
        )
        times(quad[:], pair[:, : V // 4], pair[:, V // 4 :])
        add_up(2)
        nc.vector.reciprocal(out=quad_inv[:], in_=quad[:])
        square(1)
        add_up(3)
        square(2)
        times(halves(pair_inv[:]), halves(pair[:])[:, ::-1, :], quad_inv[:].unsqueeze(1).to_broadcast([P, 2, V // 4]))
        square(3)
        times(halves(result[:, 0, :]), cofactor[:], pair_inv[:].unsqueeze(1).to_broadcast([P, 2, V // 2]))
        store(0)

        inverse = sbuf("inverse", [P, TILES, V], F32, tag="last_tanhs")
        def finish(i, cols):
            nc.scalar.activation(
                out=inverse[:, i, cols], in_=squared[:, i, cols], func=ACT.Abs_reciprocal_sqrt, scale=0.25
            )
            times(result[:, i, cols], inverse[:, i, cols], gain_t[:, cols])

        front, back = slice(0, V // 2), slice(V // 2, V)
        finish(1, front)
        finish(1, back)
        store(1)
        finish(2, slice(0, V))
        store(2)
        for cols in (front, back):
            finish(last, cols)
            store(last, cols)
